import numpy as np, ml_dtypes
CORES = [40,64,80,88,96,104,120,144]
N = 8
BF = ml_dtypes.bfloat16
F, L, W, S = 34, 96, 16, 34 * 96
def latest(gl):
    i = np.arange(L); return np.max(i - (i * np.asarray(gl).astype(np.int64)[..., None] >> 5), axis=-1)
def shortest(g1, g2):
    return latest(g1) + 1, np.maximum(latest(g2) - (L - 1), 0)
def joined(w, l1, g1, l2, g2):
    return np.concatenate([w, l1, g1, l2, g2], axis=2).astype(np.int32)
def glides(rng):
    return rng.integers(-64, 97, (N, 8, F))
def lags(rng, lo):
    hi = np.maximum(lo, np.minimum(S - 1, L * np.arange(F) + L - 1)); hi = np.where(rng.random(lo.shape) < 0.125, S - 1, hi)
    return rng.integers(lo, hi + 1)
def setup_inputs(rng):
    v = rng.integers(-127, 128, (N, 128, W * L), dtype=np.int8) >> rng.integers(0, 6, (N, 128, 1), dtype=np.int8)
    g1, g2 = glides(rng), glides(rng); m1, m2 = shortest(g1, g2)
    return {"book": v.astype(np.float32).astype(BF), "par": joined(rng.integers(0, W, (N, 8, F)), lags(rng, m1), g1, lags(rng, m2), g2)}
def setup_inputs_near(rng):
    d = setup_inputs(rng); g1, g2 = glides(rng), glides(rng); m1, m2 = shortest(g1, g2)
    l1 = np.minimum(m1 + rng.integers(0, 4, m1.shape) * (rng.random(m1.shape) < 0.5), S - 1); l2 = np.minimum(m2 + rng.integers(0, 4, m2.shape) * (rng.random(m2.shape) < 0.5), S - 1)
    d["par"] = joined(rng.integers(0, W, (N, 8, F)), l1, g1, l2, g2); return d
def setup_inputs_far(rng):
    d = setup_inputs(rng); g = [np.where(rng.random((N, 8, F)) < 0.5, 0, glides(rng)) for k in range(2)]; m = shortest(g[0], g[1]); l = []
    for k in range(2):
        a = L * np.arange(F) + rng.integers(0, L, (N, 8, F)); a = np.where(rng.random(a.shape) < 0.25, S - 1 - rng.integers(0, 2, a.shape), a)
        l.append(np.minimum(np.maximum(a, m[k]), S - 1))
    d["par"] = joined(rng.integers(0, W, (N, 8, F)), l[0], g[0], l[1], g[1]); return d
def setup_inputs_ends(rng):
    d = setup_inputs(rng); e = np.array([-64, -63, -33, -32, -31, -1, 0, 1, 31, 32, 33, 63, 64, 95, 96]); g = [rng.choice(e, (N, 8, F)) for k in range(2)]; m = shortest(g[0], g[1]); l = []
    for k in range(2):
        u = rng.random((N, 8, F)); l.append(np.where(u < 0.25, m[k], np.where(u < 0.375, S - 1, lags(rng, m[k]))))
    d["par"] = joined(rng.choice(np.array([0, W - 1, W >> 1]), (N, 8, F)), l[0], g[0], l[1], g[1]); return d
def setup_inputs_loud(rng):
    d = setup_inputs(rng); v = np.array([-127, -126, 126, 127, -1, 0, 1, 127, -127], np.float32)
    d["book"] = v[rng.integers(0, 9, (N, 128, W * L), dtype=np.int8)].astype(BF); return d
def setup_inputs_spread(rng):
    d = setup_inputs(rng); v = rng.integers(-127, 128, (N, 128, W * L), dtype=np.int8) >> rng.integers(0, 8, (N, 1, W * L), dtype=np.int8)
    d["book"] = (v * (rng.random((N, 1, W * L)) > 0.0625)).astype(np.float32).astype(BF)
    w = d["par"][:, :, :F]; d["par"][:, :, :F] = np.where(rng.random(w.shape) < 0.5, rng.integers(0, W, (N, 8, 1)), w); return d
def check_inputs(d):
    b = d["book"].astype(np.float32); p = d["par"].astype(np.int64); bad = []
    w, l1, g1, l2, g2 = [p[:, :, F * k:F * k + F] for k in range(5)]
    if not ((b == np.floor(b)) & (np.abs(b) <= 127)).all(): bad.append("book")
    if not ((w >= 0) & (w < W)).all(): bad.append("words")
    if not ((l1 >= 0) & (l1 < S) & (l2 >= 0) & (l2 < S)).all(): bad.append("lags")
    if not ((g1 >= -64) & (g1 <= 96) & (g2 >= -64) & (g2 <= 96)).all(): bad.append("glides")
    if not (latest(g1) - l1 < 0).all(): bad.append("own_places")
    if not (latest(g2) - l2 < L).all(): bad.append("lower_places")
    return bad
def reference(book, par):
    w, l1, g1, l2, g2 = [par[:, :, F * k:F * k + F].astype(np.int64) for k in range(5)]
    x = np.zeros((N + 1, 8, 16, S + 1), np.float32); i = np.arange(L)
    for r in range(N):
        b = book[r].astype(np.float32).reshape(8, 16, W, L)
        for k in range(F):
            own = np.maximum(L * k + i - l1[r, :, k, None] - (i * g1[r, :, k, None] >> 5), -1) + 1
            low = np.maximum(L * k + i - l2[r, :, k, None] - (i * g2[r, :, k, None] >> 5), -1) + 1
            for g in range(8):
                v = b[g, :, w[r, g, k]] + x[r + 1, g][:, own[g]] - x[r, g][:, low[g]]
                x[r + 1, g, :, L * k + 1:L * k + L + 1] = np.minimum(np.maximum(v, np.float32(-127)), np.float32(127))
    return {"y": np.ascontiguousarray(x[1:, :, :, 1:]).reshape(N, 128, S)}

@@ -1,0 +1,440 @@
+from concourse.bass import DstId, RemoteDMATransfer
+from concourse.mybir import AluOpType as A, ActivationFunctionType as AF
+
+N, F, L, NW = 8, 34, 96, 16
+SKEW = 2
+OFF_LOW, OFF_B = 1, 2
+OPS = [("D", True, 0, 4), ("A", True, 4, 6), ("A", False, 6, 14), ("D", False, 14, 18)]
+ROUNDS = [11, 12, 5, 2]
+NSTEP = F + SKEW * (N - 1)
+LEAD = OFF_B
+NE = NSTEP + LEAD
+ZB, ZP = NW * L, 864
+XB = ZB + 4 * ZP
+MID = 1632
+MAGIC = 12582912.0
+NPX = 4
+NR, TOP = len(ROUNDS), N - 1
+WA, WB = L * SKEW // 4, L * SKEW // 8
+SELA, SELB = 4 * 16 * (TOP - 1) - 4, 8 * 16 * TOP - 8
+
+
+def _frames(k, r):
+    extra = SKEW * min(TOP - r, 2)
+    return (0, ROUNDS[0] + extra) if k == 0 else (sum(ROUNDS[:k]) + extra, ROUNDS[k])
+
+
+def _tiles():
+    place, fill = {}, [0, 0]
+    for k in sorted(range(len(OPS)), key=lambda k: -(OPS[k][3] - OPS[k][2]) - (0 if OPS[k][1] else 100)):
+        w = (OPS[k][3] - OPS[k][2]) * NE
+        b = 0 if fill[0] + w <= 512 else 1
+        place[k] = (b, fill[b])
+        fill[b] += w
+    return place, fill
+
+
+PLACE, FILL = _tiles()
+
+SCRATCH = {
+    "pst": ("dram", [128, 17], "int32"), "pl": ("dram", [N, 128, 17], "int32"),
+    "bst": ("dram", [N, 128, 192], "bfloat16"), "bl": ("dram", [N, 128, 192], "bfloat16"),
+    "rb": ("dram", [128, 192], "bfloat16"),
+    "win": ("sbuf", [128, XB + L * NSTEP], "bfloat16"),
+    "gat": ("sbuf", [128, 288 * NE], "bfloat16"),
+    "off": ("sbuf", [128, 1024], "uint16"),
+    "pc": ("sbuf", [128, 4], "int32"), "m16": ("sbuf", [128, 8], "float32"),
+    "rr": ("sbuf", [128, 128], "float32"), "ee": ("sbuf", [128, 128], "float32"), "qq": ("sbuf", [128, 128], "float32"),
+    "ci": ("sbuf", [128, 8], "int32"), "col": ("sbuf", [128, 16], "float32"), "cm": ("sbuf", [128, 16], "float32"),
+    "tt": ("sbuf", [128, 4], "float32"), "sk": ("sbuf", [128, 4], "uint16"),
+    "ps": ("sbuf", [128, 40], "int32"), "rm": ("sbuf", [128, 64], "float16"),
+    "crow": ("sbuf", [128, 1024], "float32"), "ones": ("sbuf", [128, 128], "float32"),
+    "y0": ("sbuf", [128, 256], "float32"), "nb": ("sbuf", [128, 256], "float32"), "uu": ("sbuf", [128, 256], "bfloat16"),
+    "wt": ("sbuf", [128, 13 * 128], "float16"),
+    "ident": ("sbuf", [128, 128], "bfloat16"), "shift": ("sbuf", [128, 128], "bfloat16"),
+    "zz": ("sbuf", [128, 272], "float32"), "sel": ("sbuf", [128, 272], "bfloat16"),
+    "fina": ("sbuf", [128, WA], "float32"), "rfa": ("dram", [128, WA], "float32"), "fla": ("dram", [N, 128, WA], "float32"),
+    "finb": ("sbuf", [128, WB], "float32"), "rfb": ("dram", [128, WB], "float32"), "flb": ("dram", [N, 128, WB], "float32"),
+    "po0": ("psum", [128, 512], "float32"), "po1": ("psum", [128, 512], "float32"),
+}
+for _k in range(NPX):
+    SCRATCH["px%d" % _k] = ("psum", [128, 512], "float32")
+for _k in range(NR):
+    for _r in range(N):
+        _n = _frames(_k, _r)[1]
+        SCRATCH["ost%d_%d" % (_k, _n)] = ("dram", [N, 128, 12 * _n], "bfloat16")
+        SCRATCH["ol%d_%d" % (_k, _n)] = ("dram", [N, 128, 12 * _n], "bfloat16")
+        SCRATCH["ro%d_%d" % (_k, _n)] = ("dram", [128, 12 * _n], "bfloat16")
+
+SEMAPHORES = (["ls", "pp", "bf", "bn", "pa", "ban", "baf", "rp", "rbk", "plo", "blo", "gi1", "gi2", "gi3", "vs", "z0", "z1", "rg",
+               "pf0", "pf1", "of0", "of1", "cl", "pe", "st", "mma", "mmb", "cpa", "cpb", "rsa", "rsb", "faa", "fab", "stf"]
+              + ["g%d_%d" % (k, j) for k in range(len(OPS)) for j in range(3)]
+              + ["%s%d" % (s, k) for s in ("so", "oa", "rk") for k in range(NR)])
+
+
+def _mask(es):
+    return sum(1 << int(e) for e in es)
+
+
+def _plan(T, topo):
+    near, far = {}, {}
+    for r, c in enumerate(T.cores):
+        near[r] = [d for d in range(N) if d != r and topo.may_write(c, T.cores[d])]
+        far[r] = {}
+        used = []
+        for d in range(N):
+            if d == r or d in near[r]:
+                continue
+            h = [x for x in topo.cores_of(c) if x not in T.cores and topo.may_write(x, T.cores[d])]
+            h.sort(key=lambda x: used.count(x))
+            far[r][d] = h[0]
+            used.append(h[0])
+    return near, far
+
+
+def _runs(xs):
+    out = []
+    for x in sorted(xs):
+        if out and out[-1][1] == x:
+            out[-1][1] = x + 1
+        else:
+            out.append([x, x + 1])
+    return out
+
+
+def _xfer(topo, src, dst, es, sem, s_ap, d_ap):
+    rid, pid = topo.addr(dst, src)
+    return RemoteDMATransfer(dst_ids=[DstId(rid=rid, pnc=pid)], dma_engine_mask=_mask(es), remote_sem=sem, src=s_ap, dst=d_ap)
+
+
+def _buf(T, kind, k, r):
+    return T["%s%d_%d" % (kind, k, _frames(k, r)[1])]
+
+
+def relay_program(g, core, T, topo, r, d):
+    S, dst = T.sem, T.cores[d]
+    rid, pid = topo.addr(dst, core)
+    m, ne = topo.mask(core, dst), len(topo.engines(core, dst))
+    n_in = len(topo.engines(T.cores[r], core))
+    jobs = [(S.rp, 2, T.pst[:], T.pl[r], S.pa), (S.rbk, 4, T.rb[:], T.bl[r], S.baf)]
+    jobs += [(S["rk%d" % k], 2, _buf(T, "ro", k, d)[:], _buf(T, "ol", k, d)[r], S["oa%d" % k]) for k in range(NR)]
+    if d >= TOP - 1:
+        jobs.insert(len(jobs) - 1, (S.rsa, n_in - ne, T.rfa[:], T.fla[r], S.faa))
+    if d == TOP:
+        jobs.append((S.rsb, n_in, T.rfb[:], T.flb[r], S.fab))
+    for sem, cnt, s_ap, d_ap, rsem in jobs:
+        g.wait_ge(sem, cnt)
+        g.remote_dma(d_ap, s_ap, rsem, S.ls, pid, rid, m)
+    g.wait_ge(S.ls, ne * len(jobs))
+
+
+def rank_program(g, core, T, topo):
+    near, far = _plan(T, topo)
+    rank = T.rank_of(core)
+    if rank is None:
+        for r in range(N):
+            for d, h in far[r].items():
+                if h == core:
+                    relay_program(g, core, T, topo, r, d)
+        return
+    S, V, ACT, PE, SP = T.sem, g.vector, g.scalar, g.tensor, g.sync
+    me, nr, fr = rank, near[rank], sorted(far[rank])
+    e_off = topo.engines(core, T.cores[nr[0]])
+    e_all = topo.engines(core, far[me][fr[0]])
+    e_on = [e for e in e_all if e not in e_off]
+    from_far = [r for r in range(N) if me in far[r]]
+    from_near = [r for r in range(N) if me in near[r]]
+    n_far = sum(len(topo.engines(far[r][me], core)) for r in from_far)
+    n_near = sum(len(topo.engines(T.cores[r], core)) for r in from_near)
+    row0 = min(5 * me, 24)
+    o = 5 * me - row0
+    ls = [0]
+
+    def send(dests, near_es, far_es, src_of, near_dst, near_sem, far_dst, far_sem):
+        tr = []
+        for d in dests:
+            if d in nr:
+                es = near_es(d)
+                tr.append(_xfer(topo, core, T.cores[d], es, near_sem, src_of(d), near_dst))
+            elif d in fr:
+                es = far_es(d)
+                tr.append(_xfer(topo, core, far[me][d], es, far_sem, src_of(d), far_dst))
+            else:
+                continue
+            ls[0] += len(es)
+        if tr:
+            g.remote_dma_fused(tr, local_sem=S.ls)
+
+    def two_off(d):
+        return e_off[2 * nr.index(d):2 * nr.index(d) + 2]
+
+    def two_on(d):
+        return e_on[2 * fr.index(d):2 * fr.index(d) + 2]
+
+    def four_all(d):
+        return e_all[4 * fr.index(d):4 * fr.index(d) + 4]
+
+    SP.dma_start(T.pst[0:80, :], T.par[:]).then_inc(S.pp, 16)
+    ACT.dma_start(T.pst[80:128, :], T.par[:, 0:102]).then_inc(S.pp, 16)
+    qs = [SP, ACT]
+    fruns, nruns = _runs(fr), _runs(nr)
+    for i, (a, b) in enumerate(fruns):
+        qs[i % 2].dma_start(T.bst[a:b], T.book[16 * a:16 * b, :]).then_inc(S.bf, 16)
+    ACT.dma_start(T.pl[me, 0:80, :], T.par[:]).then_inc(S.pa, 16)
+    for i, (a, b) in enumerate(nruns):
+        qs[i % 2].dma_start(T.bst[a:b], T.book[16 * a:16 * b, :]).then_inc(S.bn, 16)
+    ACT.dma_start(T.win[16 * me:16 * me + 16, 0:ZB], T.book[16 * me:16 * me + 16, :]).then_inc(S.blo, 16)
+    nblo = 16
+
+    fl = {"allow_small_or_imprecise_dtypes": True}
+    g.iota(T.pc[:], [[16, 4]], 0, 1).then_inc(S.gi1, 1)
+    g.iota(T.m16[:], [[16, 8]], 0, 0, **fl).then_inc(S.gi1, 1)
+    g.iota(T.ee[:], [[1, 128]], 0, -1, **fl).then_inc(S.gi2, 1)
+    g.iota(T.rr[:], [[1, 8], [0, 16]], 0, 0, **fl).then_inc(S.gi2, 1)
+    g.iota(T.qq[:], [[0, 8], [1, 16]], 0, 0, **fl).then_inc(S.gi2, 1)
+    g.wait_ge(S.pp, 32)
+    send(range(N), two_off, two_on, lambda d: T.pst[:], T.pl[me], S.pa, T.pst[:], S.rp)
+    g.wait_ge(S.bf, 16 * len(fruns))
+    send(fr, None, four_all, lambda d: T.bst[d], None, None, T.rb[:], S.rbk)
+    g.wait_ge(S.bn, 16 * len(nruns))
+    send(nr, two_off, None, lambda d: T.bst[d], T.bl[me], S.ban, None, None)
+    g.iota(T.zz[:, 0:136], [[1, 136]], SELA, -4, **fl).then_inc(S.gi3, 1)
+    g.iota(T.zz[:, 136:272], [[1, 136]], SELB, -8, **fl).then_inc(S.gi3, 1)
+
+    vs = [0]
+
+    def inc(ins):
+        ins.then_inc(S.vs, 1)
+        vs[0] += 1
+
+    def phase():
+        V.wait_ge(S.vs, vs[0])
+        return vs[0]
+
+    def ts(out, in0, s1, op0, s2=None, op1=None):
+        if op1 is None:
+            inc(V.tensor_scalar(out, in0, s1, None, op0))
+        else:
+            inc(V.tensor_scalar(out, in0, s1, s2, op0, op1))
+
+    def c(j):
+        return T.col[:, j:j + 1]
+
+    RF, RM1, RC, MQ, C1O, C2O, C1L, C2L, N16, N96, SUB = range(11)
+    V.memset(T.win[:, ZB:ZB + ZP], 0.0).then_inc(S.z0, 1)
+    inc(V.memset(T.ones[0:1, :], 1.0))
+    V.wait_ge(S.gi1, 2)
+    qi, ri = T.ci[:, 0:1], T.ci[:, 1:2]
+    ts(qi, T.pc[:, 0:1], 15, A.bitwise_and)
+    ts(ri, T.pc[:, 0:1], 4, A.arith_shift_right)
+    phase()
+    ts(c(RF), ri, 0.0, A.add)
+    ts(c(RM1), ri, -1.0, A.add)
+    ts(c(RC), ri, float(16 + SKEW), A.mult, float(LEAD - 4), A.add)
+    ts(c(MQ), qi, -1.0, A.mult, MAGIC, A.add)
+    ts(c(C1O), qi, float(o + 2), A.is_equal, -1.0 / 32, A.mult)
+    ts(c(C2O), qi, float(o + 1), A.is_equal, -1.0, A.mult)
+    ts(c(C1L), qi, float(o + 4), A.is_equal, -1.0 / 32, A.mult)
+    ts(c(C2L), qi, float(o + 3), A.is_equal, -1.0, A.mult)
+    ts(c(N16), qi, float(o), A.is_equal, float(NW), A.mult)
+    ts(c(N96), qi, float(o), A.is_equal, float(L), A.mult)
+    phase()
+    V.wait_ge(S.gi2, 3)
+    cols = []
+    for k, (eng, crit, u0, u1) in enumerate(OPS):
+        b, c0 = PLACE[k]
+        for u in range(u0, u1):
+            cols.append((u // 6, u % 6, (0, OFF_LOW, OFF_B)[u // 6], b, c0 + u - u0, u1 - u0))
+    for li, m, ahead, b, c0, w in cols:
+        base = 16 * m + 31.0 / 64
+        if li < 2:
+            base += XB - MID + L * (ahead - LEAD - SKEW * li)
+        c1 = 512 * b + c0
+        ts(T.crow[0:1, c1:c1 + w * (NE - 1) + 1:w], T.ee[0:1, 0:NE], float(L if li < 2 else 0), A.mult, base, A.add)
+    ts(c(SUB), c(C2O), c(C2L), A.add, float(-MID), A.mult)
+    ts(T.tt[:], T.pc[:], c(RC), A.subtract)
+    ts(T.cm[:, 0:8], T.m16[:], c(C1O), A.mult)
+    ts(T.cm[:, 8:16], T.m16[:], c(C1L), A.mult)
+    ts(T.y0[:, 0:128], T.qq[:], c(C1O), A.mult, c(C2O), A.add)
+    ts(T.y0[:, 128:256], T.qq[:], c(C1L), A.mult, c(C2L), A.add)
+    ts(T.nb[:, 0:128], T.rr[:], c(RF), A.not_equal, 1024.0, A.mult)
+    ts(T.nb[:, 128:256], T.rr[:], c(RM1), A.not_equal, 1024.0, A.mult)
+    v_crow = phase()
+    V.wait_ge(S.z0, 1)
+    ts(T.sk[:], T.tt[:], 3.0, A.max, 38.0, A.min)
+    ts(T.ps[:], T.win[:, ZB:ZB + 40], c(N16), A.add, c(SUB), A.add)
+    inc(V.tensor_tensor(T.uu[:], T.y0[:], T.nb[:], A.add))
+    v_ps = phase()
+    for li in range(2):
+        for m in range(6):
+            j = 6 * li + m
+            ts(T.wt[:, 128 * j:128 * j + 128], T.uu[:, 128 * li:128 * li + 128], T.cm[:, 8 * li + m:8 * li + m + 1], A.add, 0.0, A.min)
+    ts(T.wt[:, 128 * 12:128 * 13], T.rr[:], c(RF), A.is_equal, c(N96), A.mult)
+    ts(T.ident[:], T.ee[:], 0.0, A.is_equal)
+    ts(T.shift[:], T.ee[:], 16.0, A.is_equal, -1.0, A.mult)
+    V.wait_ge(S.gi3, 2)
+    ts(T.sel[:], T.zz[:], 0.0, A.is_equal)
+    v_all = phase()
+
+    ACT.wait_ge(S.z0, 1)
+    for j in range(1, 4):
+        ACT.activation(T.win[:, ZB + j * ZP:ZB + (j + 1) * ZP], T.win[:, ZB:ZB + ZP], AF.Copy).then_inc(S.z1, 1)
+
+    SP.wait_ge(S.vs, v_ps)
+    SP.wait_ge(S.pa, 16 + 2 * len(from_near) + n_far)
+    SP.dma_start(T.ps[:, 4:38], T.pl[:, 2 * row0:2 * row0 + 32, :]).then_inc(S.plo, 16)
+    ACT.wait_ge(S.ban, 2 * len(from_near))
+    for a, b in _runs(from_near):
+        ACT.dma_start(T.win[16 * a:16 * b, 0:ZB], T.bl[a:b]).then_inc(S.blo, 16)
+        nblo += 16
+    ACT.wait_ge(S.baf, n_far)
+    SP.wait_ge(S.baf, n_far)
+    for i, (a, b) in enumerate(_runs(from_far)):
+        [SP, ACT][i % 2].dma_start(T.win[16 * a:16 * b, 0:ZB], T.bl[a:b]).then_inc(S.blo, 16)
+        nblo += 16
+
+    po = [T.po0, T.po1]
+    PE.wait_ge(S.vs, v_crow)
+    for b in range(2):
+        PE.matmul(po[b][:, 0:FILL[b]], T.ones[0:1, :], T.crow[0:1, 512 * b:512 * b + FILL[b]], True, False)
+    V.wait_ge(S.plo, 16)
+    V.tensor_scalar(T.rm[:], T.ps[:, 0:40].indirect(T.sk[:, 0:4]), c(SUB), None, A.subtract).then_inc(S.rg, 1)
+    PE.wait_ge(S.vs, v_all)
+    PE.wait_ge(S.rg, 1)
+    for b in range(2):
+        mine = [x for x in cols if x[3] == b]
+        for i, (li, m, ahead, _b, c0, w) in enumerate(mine):
+            j = 12 if li == 2 else 6 * li + m
+            ins = PE.matmul(po[b][:, c0:c0 + w * (NE - 1) + 1:w], T.wt[:, 128 * j:128 * j + 128], T.rm[:, ahead:ahead + NE],
+                            False, i == len(mine) - 1)
+        ins.then_inc(S["pf%d" % b], 1)
+    for b in range(2):
+        V.wait_ge(S["pf%d" % b], 1)
+        V.tensor_scalar(T.off[:, 512 * b:512 * b + FILL[b]], po[b][:, 0:FILL[b]], MAGIC, c(MQ), A.add, A.subtract).then_inc(S["of%d" % b], 1)
+
+    Q = {"D": V, "A": ACT}
+    seen = {"D": [], "A": []}
+    for q in (V, ACT):
+        q.wait_ge(S.z1, 3)
+        q.wait_ge(S.blo, nblo)
+    cnt = {}
+
+    def needed(k, e):
+        eng, crit, u0, u1 = OPS[k]
+        return any(0 <= e + (0, OFF_LOW, OFF_B)[u // 6] < NSTEP for u in range(u0, u1))
+
+    def gather(k, e):
+        eng, crit, u0, u1 = OPS[k]
+        b, c0 = PLACE[k]
+        if b not in seen[eng]:
+            Q[eng].wait_ge(S["of%d" % b], 1)
+            seen[eng].append(b)
+        w, t = u1 - u0, e + LEAD
+        src = T.win[:, 0:XB + L * max(e, 0)].indirect(T.off[:, 512 * b + c0 + w * t:512 * b + c0 + w * (t + 1)])
+        out = T.gat[:, 288 * t + 16 * u0:288 * t + 16 * u1]
+        ins = V.tensor_copy(out, src) if eng == "D" else ACT.activation(out, src, AF.Copy)
+        name = "g%d_%d" % (k, t % 3)
+        ins.then_inc(S[name], 1)
+        cnt[name] = cnt.get(name, 0) + 1
+        cnt[(k, e)] = (name, cnt[name])
+
+    waited = {}
+
+    def sum_in(s, li, first, last):
+        e = s - (0, OFF_LOW, OFF_B)[li]
+        for k, (eng, crit, u0, u1) in enumerate(OPS):
+            if u0 < 6 * li + 6 and u1 > 6 * li and (k, e) not in waited:
+                PE.wait_ge(S[cnt[(k, e)][0]], cnt[(k, e)][1])
+                waited[(k, e)] = True
+        c0 = 288 * (e + LEAD) + L * li
+        return PE.matmul(T["px%d" % (s % NPX)][:, 0:L], (T.shift if li == 1 else T.ident)[:], T.gat[:, c0:c0 + L], first, last)
+
+    def spread(done, parts, sel0, bank, w, sem):
+        PE.wait_ge(S.cl, done)
+        c0 = XB + L * (done - SKEW)
+        for j in range(parts):
+            ins = PE.matmul(bank[:, 0:w], T.sel[:, sel0 + parts - j:sel0 + parts - j + 128], T.win[:, c0 + w * j:c0 + w * (j + 1)],
+                            j == 0, j == parts - 1)
+        ins.then_inc(sem, 1)
+
+    order = [2, 1, 0] if OFF_LOW else [2, 0, 1]
+    for e in range(-LEAD, NSTEP):
+        if e > 0:
+            V.wait_ge(S.cl, e)
+            ACT.wait_ge(S.cl, e)
+        for k in range(len(OPS)):
+            if needed(k, e):
+                gather(k, e)
+        if e == NSTEP - SKEW + 1:
+            V.wait_ge(S.mma, 1)
+            V.tensor_copy(T.fina[:], T.po1[:, 0:WA]).then_inc(S.cpa, 1)
+        if e >= 0:
+            for i, li in enumerate(order):
+                ins = sum_in(e, li, i == 0, i == 2)
+            ins.then_inc(S.pe, 1)
+            if e == NSTEP - SKEW:
+                spread(e, 4, 0, T.po1, WA, S.mma)
+            V.wait_ge(S.pe, e + 1)
+            V.tensor_scalar(T.win[:, XB + L * e:XB + L * e + L], T["px%d" % (e % NPX)][:, 0:L], 127.0, -127.0, A.min, A.max).then_inc(S.cl, 1)
+    spread(NSTEP, 8, 136, T.po0, WB, S.mmb)
+    V.wait_ge(S.mmb, 1)
+    V.tensor_copy(T.finb[:], T.po0[:, 0:WB]).then_inc(S.cpb, 1)
+
+    jobs = sorted((sum(_frames(k, r)) + SKEW * r, k, r) for k in range(NR) for r in range(N))
+    last = 0
+    for done, k, r in jobs:
+        if done > last:
+            SP.wait_ge(S.cl, done)
+            last = done
+        f0, n = _frames(k, r)
+        c0 = XB + L * (f0 + SKEW * r)
+        out = _buf(T, "ol", k, r)[me] if r == me else _buf(T, "ost", k, r)[r]
+        SP.dma_start(out, T.win[16 * r:16 * r + 16, c0:c0 + L * n]).then_inc(S["so%d" % k], 16)
+
+    def round_out(k):
+        g.wait_ge(S["so%d" % k], 16 * N)
+        for n in sorted(set(_frames(k, r)[1] for r in range(N))):
+            ds = [r for r in range(N) if _frames(k, r)[1] == n]
+            send(ds, two_off, two_on, lambda d: _buf(T, "ost", k, d)[d], _buf(T, "ol", k, ds[0])[me], S["oa%d" % k],
+                 _buf(T, "ro", k, ds[0])[:], S["rk%d" % k])
+
+    def store(k):
+        f0, n = _frames(k, me)
+        g.wait_ge(S["oa%d" % k], 2 * len(from_near) + n_far)
+        g.dma_start(T.y[:, L * f0:L * (f0 + n)], _buf(T, "ol", k, me)[:]).then_inc(S.st, 16)
+
+    round_out(0)
+    round_out(1)
+    store(0)
+    for k in range(2, NR - 1):
+        round_out(k)
+    g.wait_ge(S.cpa, 1)
+    send([TOP - 1, TOP], lambda d: e_off, lambda d: e_on, lambda d: T.fina[:], T.fla[me], S.faa, T.rfa[:], S.rsa)
+    round_out(NR - 1)
+    if me != TOP:
+        g.wait_ge(S.cpb, 1)
+        send([TOP], lambda d: e_off, lambda d: e_all, lambda d: T.finb[:], T.flb[me], S.fab, T.rfb[:], S.rsb)
+    for k in range(1, NR):
+        store(k)
+    g.wait_ge(S.ls, ls[0])
+    g.wait_ge(S.st, 16 * NR)
+
+    nst = [0]
+
+    def final(cp, fin, land, sem, p0, p1, f0):
+        t0, t1 = L * f0, L * (f0 + SKEW)
+        SP.wait_ge(cp, 1)
+        SP.dma_start(T.y[16 * me:16 * me + 16, t0:t1], fin[p0:p1, :]).then_inc(S.stf, 16)
+        SP.wait_ge(sem, n_near + n_far)
+        runs = _runs([r for r in range(N) if r != me])
+        for a, b in runs:
+            SP.dma_start(T.y[16 * a:16 * b, t0:t1], land[a:b, p0:p1, :]).then_inc(S.stf, 16)
+        nst[0] += 16 * (1 + len(runs))
+
+    if me == TOP - 1:
+        final(S.cpa, T.fina, T.fla, S.faa, 0, 64, F - SKEW)
+    if me == TOP:
+        final(S.cpa, T.fina, T.fla, S.faa, 64, 128, F - 2 * SKEW)
+        final(S.cpb, T.finb, T.flb, S.fab, 0, 128, F - SKEW)
+    if nst[0]:
+        SP.wait_ge(S.stf, nst[0])

@@ -4,19 +4,21 @@ from concourse.mybir import AluOpType as A, ActivationFunctionType as AF
 N, F, L, NW = 8, 34, 96, 16
 SKEW = 2
 OFF_LOW, OFF_B = 1, 2
-OPS = [("D", True, 0, 4), ("A", True, 4, 6), ("A", False, 6, 14), ("D", False, 14, 18)]
+OPS = [("D", True, 0, 6), ("A", False, 6, 12), ("A", False, 12, 18)]
 ROUNDS = [11, 12, 5, 2]
 NSTEP = F + SKEW * (N - 1)
 LEAD = OFF_B
 NE = NSTEP + LEAD
 ZB, ZP = NW * L, 864
 XB = ZB + 4 * ZP
+UB = 4 * ZP
 MID = 1632
 MAGIC = 12582912.0
 NPX = 4
 NR, TOP = len(ROUNDS), N - 1
 WA, WB = L * SKEW // 4, L * SKEW // 8
 SELA, SELB = 4 * 16 * (TOP - 1) - 4, 8 * 16 * TOP - 8
+PLACE, FILL = {0: (2, 0), 1: (1, 0), 2: (0, 0)}, [6 * NE] * 3
 
 
 def _frames(k, r):
@@ -24,38 +26,26 @@ def _frames(k, r):
     return (0, ROUNDS[0] + extra) if k == 0 else (sum(ROUNDS[:k]) + extra, ROUNDS[k])
 
 
-def _tiles():
-    place, fill = {}, [0, 0]
-    for k in sorted(range(len(OPS)), key=lambda k: -(OPS[k][3] - OPS[k][2]) - (0 if OPS[k][1] else 100)):
-        w = (OPS[k][3] - OPS[k][2]) * NE
-        b = 0 if fill[0] + w <= 512 else 1
-        place[k] = (b, fill[b])
-        fill[b] += w
-    return place, fill
-
-
-PLACE, FILL = _tiles()
-
 SCRATCH = {
     "pst": ("dram", [128, 17], "int32"), "pl": ("dram", [N, 128, 17], "int32"),
     "bst": ("dram", [N, 128, 192], "bfloat16"), "bl": ("dram", [N, 128, 192], "bfloat16"),
     "rb": ("dram", [128, 192], "bfloat16"),
     "win": ("sbuf", [128, XB + L * NSTEP], "bfloat16"),
     "gat": ("sbuf", [128, 288 * NE], "bfloat16"),
-    "off": ("sbuf", [128, 1024], "uint16"),
+    "off": ("sbuf", [128, 1536], "uint16"), "uw": ("sbuf", [128, UB + L * NSTEP], "bfloat16"),
     "pc": ("sbuf", [128, 4], "int32"), "m16": ("sbuf", [128, 8], "float32"),
     "rr": ("sbuf", [128, 128], "float32"), "ee": ("sbuf", [128, 128], "float32"), "qq": ("sbuf", [128, 128], "float32"),
     "ci": ("sbuf", [128, 8], "int32"), "col": ("sbuf", [128, 16], "float32"), "cm": ("sbuf", [128, 16], "float32"),
     "tt": ("sbuf", [128, 4], "float32"), "sk": ("sbuf", [128, 4], "uint16"),
     "ps": ("sbuf", [128, 40], "int32"), "rm": ("sbuf", [128, 64], "float16"),
-    "crow": ("sbuf", [128, 1024], "float32"), "ones": ("sbuf", [128, 128], "float32"),
+    "crow": ("sbuf", [128, 1536], "float32"), "ones": ("sbuf", [128, 128], "float32"),
     "y0": ("sbuf", [128, 256], "float32"), "nb": ("sbuf", [128, 256], "float32"), "uu": ("sbuf", [128, 256], "bfloat16"),
     "wt": ("sbuf", [128, 13 * 128], "float16"),
     "ident": ("sbuf", [128, 128], "bfloat16"), "shift": ("sbuf", [128, 128], "bfloat16"),
     "zz": ("sbuf", [128, 272], "float32"), "sel": ("sbuf", [128, 272], "bfloat16"),
     "fina": ("sbuf", [128, WA], "float32"), "rfa": ("dram", [128, WA], "float32"), "fla": ("dram", [N, 128, WA], "float32"),
     "finb": ("sbuf", [128, WB], "float32"), "rfb": ("dram", [128, WB], "float32"), "flb": ("dram", [N, 128, WB], "float32"),
-    "po0": ("psum", [128, 512], "float32"), "po1": ("psum", [128, 512], "float32"),
+    "po0": ("psum", [128, 512], "float32"), "po1": ("psum", [128, 512], "float32"), "po2": ("psum", [128, 512], "float32"),
 }
 for _k in range(NPX):
     SCRATCH["px%d" % _k] = ("psum", [128, 512], "float32")
@@ -67,7 +57,8 @@ for _k in range(NR):
         SCRATCH["ro%d_%d" % (_k, _n)] = ("dram", [128, 12 * _n], "bfloat16")
 
 SEMAPHORES = (["ls", "pp", "bf", "bn", "pa", "ban", "baf", "rp", "rbk", "plo", "blo", "gi1", "gi2", "gi3", "vs", "z0", "z1", "rg",
-               "pf0", "pf1", "of0", "of1", "cl", "pe", "st", "mma", "mmb", "cpa", "cpb", "rsa", "rsb", "faa", "fab", "stf"]
+               "pf0", "pf1", "pf2", "of0", "of1", "of2", "cl0", "cl1", "pe0", "pe1", "us", "st",
+               "mma", "mmb", "cpa", "cpb", "rsa", "rsb", "faa", "fab", "stf"]
               + ["g%d_%d" % (k, j) for k in range(len(OPS)) for j in range(3)]
               + ["%s%d" % (s, k) for s in ("so", "oa", "rk") for k in range(NR)])
 
@@ -248,7 +239,7 @@ def rank_program(g, core, T, topo):
     for li, m, ahead, b, c0, w in cols:
         base = 16 * m + 31.0 / 64
         if li < 2:
-            base += XB - MID + L * (ahead - LEAD - SKEW * li)
+            base += (XB if li else UB) - MID + L * (ahead - LEAD - SKEW * li)
         c1 = 512 * b + c0
         ts(T.crow[0:1, c1:c1 + w * (NE - 1) + 1:w], T.ee[0:1, 0:NE], float(L if li < 2 else 0), A.mult, base, A.add)
     ts(c(SUB), c(C2O), c(C2L), A.add, float(-MID), A.mult)
@@ -274,11 +265,14 @@ def rank_program(g, core, T, topo):
     ts(T.shift[:], T.ee[:], 16.0, A.is_equal, -1.0, A.mult)
     V.wait_ge(S.gi3, 2)
     ts(T.sel[:], T.zz[:], 0.0, A.is_equal)
+    inc(V.memset(T.uw[:, 2 * ZP:4 * ZP], 0.0))
     v_all = phase()
 
     ACT.wait_ge(S.z0, 1)
     for j in range(1, 4):
         ACT.activation(T.win[:, ZB + j * ZP:ZB + (j + 1) * ZP], T.win[:, ZB:ZB + ZP], AF.Copy).then_inc(S.z1, 1)
+    for j in range(2):
+        ACT.activation(T.uw[:, j * ZP:(j + 1) * ZP], T.win[:, ZB:ZB + ZP], AF.Copy).then_inc(S.z1, 1)
 
     SP.wait_ge(S.vs, v_ps)
     SP.wait_ge(S.pa, 16 + 2 * len(from_near) + n_far)
@@ -293,30 +287,30 @@ def rank_program(g, core, T, topo):
         [SP, ACT][i % 2].dma_start(T.win[16 * a:16 * b, 0:ZB], T.bl[a:b]).then_inc(S.blo, 16)
         nblo += 16
 
-    po = [T.po0, T.po1]
+    po = [T.po0, T.po1, T.po2]
     PE.wait_ge(S.vs, v_crow)
-    for b in range(2):
+    for b in range(3):
         PE.matmul(po[b][:, 0:FILL[b]], T.ones[0:1, :], T.crow[0:1, 512 * b:512 * b + FILL[b]], True, False)
     V.wait_ge(S.plo, 16)
     V.tensor_scalar(T.rm[:], T.ps[:, 0:40].indirect(T.sk[:, 0:4]), c(SUB), None, A.subtract).then_inc(S.rg, 1)
     PE.wait_ge(S.vs, v_all)
     PE.wait_ge(S.rg, 1)
-    for b in range(2):
+    for b in range(3):
         mine = [x for x in cols if x[3] == b]
         for i, (li, m, ahead, _b, c0, w) in enumerate(mine):
             j = 12 if li == 2 else 6 * li + m
             ins = PE.matmul(po[b][:, c0:c0 + w * (NE - 1) + 1:w], T.wt[:, 128 * j:128 * j + 128], T.rm[:, ahead:ahead + NE],
                             False, i == len(mine) - 1)
         ins.then_inc(S["pf%d" % b], 1)
-    for b in range(2):
+    for b in range(3):
         V.wait_ge(S["pf%d" % b], 1)
         V.tensor_scalar(T.off[:, 512 * b:512 * b + FILL[b]], po[b][:, 0:FILL[b]], MAGIC, c(MQ), A.add, A.subtract).then_inc(S["of%d" % b], 1)
 
     Q = {"D": V, "A": ACT}
     seen = {"D": [], "A": []}
     for q in (V, ACT):
-        q.wait_ge(S.z1, 3)
-        q.wait_ge(S.blo, nblo)
+        q.wait_ge(S.z1, 5)
+    ACT.wait_ge(S.blo, nblo)
     cnt = {}
 
     def needed(k, e):
@@ -330,15 +324,24 @@ def rank_program(g, core, T, topo):
             Q[eng].wait_ge(S["of%d" % b], 1)
             seen[eng].append(b)
         w, t = u1 - u0, e + LEAD
-        src = T.win[:, 0:XB + L * max(e, 0)].indirect(T.off[:, 512 * b + c0 + w * t:512 * b + c0 + w * (t + 1)])
+        src = (T.uw[:, 0:UB + L * e] if crit else T.win[:, 0:XB + L * max(e, 0)]).indirect(
+            T.off[:, 512 * b + c0 + w * t:512 * b + c0 + w * (t + 1)])
         out = T.gat[:, 288 * t + 16 * u0:288 * t + 16 * u1]
-        ins = V.tensor_copy(out, src) if eng == "D" else ACT.activation(out, src, AF.Copy)
+        ins = V.tensor_scalar(out, src, 127.0, -127.0, A.min, A.max) if eng == "D" else ACT.activation(out, src, AF.Copy)
         name = "g%d_%d" % (k, t % 3)
         ins.then_inc(S[name], 1)
         cnt[name] = cnt.get(name, 0) + 1
         cnt[(k, e)] = (name, cnt[name])
 
     waited = {}
+
+    def wait_x(q, done, both=True):
+        for s in range(max(done - 2, 0) if both else done - 1, done):
+            q.wait_ge(S["cl%d" % (s % 2)], s // 2 + 1)
+
+    def bound(s):
+        V.tensor_scalar(T.win[:, XB + L * s:XB + L * s + L], T.uw[:, UB + L * s:UB + L * s + L], 127.0, -127.0,
+                        A.min, A.max).then_inc(S["cl%d" % (s % 2)], 1)
 
     def sum_in(s, li, first, last):
         e = s - (0, OFF_LOW, OFF_B)[li]
@@ -350,32 +353,38 @@ def rank_program(g, core, T, topo):
         return PE.matmul(T["px%d" % (s % NPX)][:, 0:L], (T.shift if li == 1 else T.ident)[:], T.gat[:, c0:c0 + L], first, last)
 
     def spread(done, parts, sel0, bank, w, sem):
-        PE.wait_ge(S.cl, done)
+        wait_x(PE, done)
         c0 = XB + L * (done - SKEW)
         for j in range(parts):
             ins = PE.matmul(bank[:, 0:w], T.sel[:, sel0 + parts - j:sel0 + parts - j + 128], T.win[:, c0 + w * j:c0 + w * (j + 1)],
                             j == 0, j == parts - 1)
         ins.then_inc(sem, 1)
 
-    order = [2, 1, 0] if OFF_LOW else [2, 0, 1]
     for e in range(-LEAD, NSTEP):
         if e > 0:
-            V.wait_ge(S.cl, e)
-            ACT.wait_ge(S.cl, e)
+            V.wait_ge(S.us, e)
+            if needed(1, e):
+                wait_x(ACT, e, False)
         for k in range(len(OPS)):
             if needed(k, e):
                 gather(k, e)
+        if e > 0:
+            bound(e - 1)
         if e == NSTEP - SKEW + 1:
             V.wait_ge(S.mma, 1)
             V.tensor_copy(T.fina[:], T.po1[:, 0:WA]).then_inc(S.cpa, 1)
-        if e >= 0:
-            for i, li in enumerate(order):
-                ins = sum_in(e, li, i == 0, i == 2)
-            ins.then_inc(S.pe, 1)
+        if 0 <= e + 1 < NSTEP:
+            sum_in(e + 1, 2, True, False)
             if e == NSTEP - SKEW:
                 spread(e, 4, 0, T.po1, WA, S.mma)
-            V.wait_ge(S.pe, e + 1)
-            V.tensor_scalar(T.win[:, XB + L * e:XB + L * e + L], T["px%d" % (e % NPX)][:, 0:L], 127.0, -127.0, A.min, A.max).then_inc(S.cl, 1)
+            sum_in(e + 1, 1, False, True).then_inc(S["pe%d" % ((e + 1) % 2)], 1)
+        if e >= 0:
+            V.wait_ge(S[cnt[(0, e)][0]], cnt[(0, e)][1])
+            V.wait_ge(S["pe%d" % (e % 2)], e // 2 + 1)
+            c0 = 288 * (e + LEAD)
+            V.tensor_tensor(T.uw[:, UB + L * e:UB + L * e + L], T.gat[:, c0:c0 + L], T["px%d" % (e % NPX)][:, 0:L], A.add).then_inc(S.us, 1)
+    V.wait_ge(S.us, NSTEP)
+    bound(NSTEP - 1)
     spread(NSTEP, 8, 136, T.po0, WB, S.mmb)
     V.wait_ge(S.mmb, 1)
     V.tensor_copy(T.finb[:], T.po0[:, 0:WB]).then_inc(S.cpb, 1)
@@ -384,7 +393,7 @@ def rank_program(g, core, T, topo):
     last = 0
     for done, k, r in jobs:
         if done > last:
-            SP.wait_ge(S.cl, done)
+            wait_x(SP, done)
             last = done
         f0, n = _frames(k, r)
         c0 = XB + L * (f0 + SKEW * r)

@@ -2,65 +2,76 @@ from concourse.bass import DstId, RemoteDMATransfer
 from concourse.mybir import AluOpType as A, ActivationFunctionType as AF
 
 N, F, L, NW = 8, 34, 96, 16
-SKEW = 2
-OFF_LOW, OFF_B = 1, 2
-OPS = [("D", True, 0, 6), ("A", False, 6, 12), ("A", False, 12, 18)]
-ROUNDS = [11, 12, 5, 2]
-NSTEP = F + SKEW * (N - 1)
-LEAD = OFF_B
-NE = NSTEP + LEAD
-ZB, ZP = NW * L, 864
-XB = ZB + 4 * ZP
-UB = 4 * ZP
+K = 4
+NSTEP = F + K * (N - 1)
+TOP = N - 1
+Z = 16
+KK = float(2 ** 24 + 2 ** 17 + 2 ** 10)
 MID = 1632
 MAGIC = 12582912.0
-NPX = 4
-NR, TOP = len(ROUNDS), N - 1
-WA, WB = L * SKEW // 4, L * SKEW // 8
-SELA, SELB = 4 * 16 * (TOP - 1) - 4, 8 * 16 * TOP - 8
-PLACE, FILL = {0: (2, 0), 1: (1, 0), 2: (0, 0)}, [6 * NE] * 3
+NPX = K + 1
+LOW = 384
+FIRST = 16
+
+WB = [0, 4, 12, 24, 40, NSTEP]
+WGO = [0, 0, 0, 2, 14]
+WLAND = [0, 0, 0, 0, 26]
+VF = 8
+OUT = [[12, 12, 12, 6, 6, 0, 0, 0], [12, 12, 12, 12, 12, 14, 10, 6], [10] * 8, [0, 0, 0, 6, 6, 6, 6, 6], [0, 0, 0, 0, 0, 4, 4, 4]]
+DIRECT = [(6, 54, 4, "po0"), (7, 54, 4, "po1"), (7, 58, 2, "pw"), (7, 60, 2, "po0")]
+NWR, NR, ND = len(WB) - 1, len(OUT), len(DIRECT)
+LAST_SLOT = max(K * r + sum(o[r] for o in OUT) for r in range(N))
+
+
+def _words(k, r):
+    f0, f1 = min(max(WB[k] - K * r, 0), F), min(max(WB[k + 1] - K * r, 0), F)
+    return f0, f1 - f0
 
 
 def _frames(k, r):
-    extra = SKEW * min(TOP - r, 2)
-    return (0, ROUNDS[0] + extra) if k == 0 else (sum(ROUNDS[:k]) + extra, ROUNDS[k])
+    return sum(o[r] for o in OUT[:k]), OUT[k][r]
 
 
 SCRATCH = {
     "pst": ("dram", [128, 17], "int32"), "pl": ("dram", [N, 128, 17], "int32"),
-    "bst": ("dram", [N, 128, 192], "bfloat16"), "bl": ("dram", [N, 128, 192], "bfloat16"),
-    "rb": ("dram", [128, 192], "bfloat16"),
-    "win": ("sbuf", [128, XB + L * NSTEP], "bfloat16"),
-    "gat": ("sbuf", [128, 288 * NE], "bfloat16"),
-    "off": ("sbuf", [128, 1536], "uint16"), "uw": ("sbuf", [128, UB + L * NSTEP], "bfloat16"),
-    "pc": ("sbuf", [128, 4], "int32"), "m16": ("sbuf", [128, 8], "float32"),
-    "rr": ("sbuf", [128, 128], "float32"), "ee": ("sbuf", [128, 128], "float32"), "qq": ("sbuf", [128, 128], "float32"),
-    "ci": ("sbuf", [128, 8], "int32"), "col": ("sbuf", [128, 16], "float32"), "cm": ("sbuf", [128, 16], "float32"),
+    "bk": ("sbuf", [128, NW * L], "bfloat16"), "wg": ("sbuf", [128, F * L], "bfloat16"),
+    "pn": ("sbuf", [128, 40], "int32"), "nb16": ("sbuf", [128, 40], "bfloat16"), "woff": ("sbuf", [128, 208], "uint16"),
+    "crow2": ("sbuf", [128, 208], "bfloat16"), "onesb": ("sbuf", [128, 128], "bfloat16"), "sel96": ("sbuf", [128, 128], "bfloat16"),
+    "uu": ("sbuf", [128, Z + L * NSTEP], "int32"), "cc": ("sbuf", [128, L * NSTEP], "float32"),
+    "wd": ("sbuf", [128, L * NSTEP], "bfloat16"), "lg": ("sbuf", [128, L * NSTEP], "bfloat16"),
+    "xw": ("sbuf", [128, L * NSTEP], "bfloat16"), "xx": ("sbuf", [128, L * NSTEP], "bfloat16"),
+    "off": ("sbuf", [128, 2 * LOW], "uint16"),
+    "pc": ("sbuf", [128, 4], "int32"), "jj": ("sbuf", [128, 136], "int32"),
+    "rr": ("sbuf", [128, 128], "int32"), "qq": ("sbuf", [128, 128], "int32"),
+    "ci": ("sbuf", [128, 8], "int32"), "col": ("sbuf", [128, 24], "float32"), "cm": ("sbuf", [128, 16], "float32"),
     "tt": ("sbuf", [128, 4], "float32"), "sk": ("sbuf", [128, 4], "uint16"),
     "ps": ("sbuf", [128, 40], "int32"), "rm": ("sbuf", [128, 64], "float16"),
-    "crow": ("sbuf", [128, 1536], "float32"), "ones": ("sbuf", [128, 128], "float32"),
-    "y0": ("sbuf", [128, 256], "float32"), "nb": ("sbuf", [128, 256], "float32"), "uu": ("sbuf", [128, 256], "bfloat16"),
-    "wt": ("sbuf", [128, 13 * 128], "float16"),
+    "crow": ("sbuf", [128, LOW], "float32"), "ones": ("sbuf", [128, 128], "float32"),
+    "y0": ("sbuf", [128, 256], "float32"), "nb": ("sbuf", [128, 256], "float32"), "wu": ("sbuf", [128, 256], "bfloat16"),
+    "wt": ("sbuf", [128, 12 * 128], "float16"),
     "ident": ("sbuf", [128, 128], "bfloat16"), "shift": ("sbuf", [128, 128], "bfloat16"),
-    "zz": ("sbuf", [128, 272], "float32"), "sel": ("sbuf", [128, 272], "bfloat16"),
-    "fina": ("sbuf", [128, WA], "float32"), "rfa": ("dram", [128, WA], "float32"), "fla": ("dram", [N, 128, WA], "float32"),
-    "finb": ("sbuf", [128, WB], "float32"), "rfb": ("dram", [128, WB], "float32"), "flb": ("dram", [N, 128, WB], "float32"),
-    "po0": ("psum", [128, 512], "float32"), "po1": ("psum", [128, 512], "float32"), "po2": ("psum", [128, 512], "float32"),
+    "sel": ("sbuf", [128, 2 * 136], "bfloat16"),
+    "po0": ("psum", [128, 512], "float32"), "po1": ("psum", [128, 512], "float32"), "pw": ("psum", [128, 512], "float32"),
 }
 for _k in range(NPX):
     SCRATCH["px%d" % _k] = ("psum", [128, 512], "float32")
-for _k in range(NR):
-    for _r in range(N):
-        _n = _frames(_k, _r)[1]
-        SCRATCH["ost%d_%d" % (_k, _n)] = ("dram", [N, 128, 12 * _n], "bfloat16")
-        SCRATCH["ol%d_%d" % (_k, _n)] = ("dram", [N, 128, 12 * _n], "bfloat16")
-        SCRATCH["ro%d_%d" % (_k, _n)] = ("dram", [128, 12 * _n], "bfloat16")
+for _r in range(N):
+    for _k in range(NWR):
+        if _words(_k, _r)[1]:
+            SCRATCH["ws%d_%d" % (_k, _words(_k, _r)[1])] = ("dram", [2 * N, 128, 12 * _words(_k, _r)[1]], "bfloat16")
+    for _k in range(NR):
+        if OUT[_k][_r]:
+            SCRATCH["os%d_%d" % (_k, OUT[_k][_r])] = ("dram", [2 * N, 128, 12 * OUT[_k][_r]], "bfloat16")
+for _t in range(ND):
+    SCRATCH["fin%d" % _t] = ("sbuf", [128, 12 * DIRECT[_t][2]], "float32")
+    SCRATCH["fl%d" % _t] = ("dram", [N, 128, 12 * DIRECT[_t][2]], "float32")
 
-SEMAPHORES = (["ls", "pp", "bf", "bn", "pa", "ban", "baf", "rp", "rbk", "plo", "blo", "gi1", "gi2", "gi3", "vs", "z0", "z1", "rg",
-               "pf0", "pf1", "pf2", "of0", "of1", "of2", "cl0", "cl1", "pe0", "pe1", "us", "st",
-               "mma", "mmb", "cpa", "cpb", "rsa", "rsb", "faa", "fab", "stf"]
-              + ["g%d_%d" % (k, j) for k in range(len(OPS)) for j in range(3)]
-              + ["%s%d" % (s, k) for s in ("so", "oa", "rk") for k in range(NR)])
+SEMAPHORES = (["ls", "pp", "pa", "rp", "plo", "pnl", "bkl", "gi1", "gi2", "vs", "nbs", "pwf", "wo1", "wo2", "rg",
+               "pf0", "pf1", "of0a", "of0b", "of1a", "of1b", "us", "vx", "st", "stf"]
+              + ["%s%d" % (s, k) for s in ("gl", "pe", "cp") for k in range(K)]
+              + ["%s%d" % (s, k) for s in ("wgd", "wsd", "wa", "wl", "rw") for k in range(NWR)]
+              + ["%s%d" % (s, k) for s in ("so", "oa", "rk") for k in range(NR)]
+              + ["%s%d" % (s, k) for s in ("mm", "fc", "rd", "fa") for k in range(ND)])
 
 
 def _mask(es):
@@ -83,6 +94,23 @@ def _plan(T, topo):
     return near, far
 
 
+def _share(es, ds):
+    per = 1
+    while ds and 2 * per * len(ds) <= len(es):
+        per *= 2
+    return {d: es[per * i:per * (i + 1)] for i, d in enumerate(ds)}
+
+
+def _deal(T, topo, near, far, r, ds):
+    c = T.cores[r]
+    e_off = topo.engines(c, T.cores[near[r][0]])
+    e_all = topo.engines(c, far[r][sorted(far[r])[0]])
+    dn, df = [d for d in ds if d in near[r]], [d for d in ds if d in far[r]]
+    out = _share(e_off, dn)
+    out.update(_share([e for e in e_all if e not in e_off] if dn else e_all, df))
+    return out
+
+
 def _runs(xs):
     out = []
     for x in sorted(xs):
@@ -98,21 +126,35 @@ def _xfer(topo, src, dst, es, sem, s_ap, d_ap):
     return RemoteDMATransfer(dst_ids=[DstId(rid=rid, pnc=pid)], dma_engine_mask=_mask(es), remote_sem=sem, src=s_ap, dst=d_ap)
 
 
-def _buf(T, kind, k, r):
-    return T["%s%d_%d" % (kind, k, _frames(k, r)[1])]
+def _wbuf(T, k, r):
+    return T["ws%d_%d" % (k, _words(k, r)[1])]
 
 
-def relay_program(g, core, T, topo, r, d):
+def _obuf(T, k, r):
+    return T["os%d_%d" % (k, OUT[k][r])]
+
+
+def _dests(k):
+    return [r for r in range(N) if OUT[k][r]]
+
+
+def _together(t):
+    return [x[0] for x in DIRECT if x[1] + x[2] == DIRECT[t][1] + DIRECT[t][2]]
+
+
+def relay_program(g, core, T, topo, near, far, r, d):
     S, dst = T.sem, T.cores[d]
     rid, pid = topo.addr(dst, core)
     m, ne = topo.mask(core, dst), len(topo.engines(core, dst))
-    n_in = len(topo.engines(T.cores[r], core))
-    jobs = [(S.rp, 2, T.pst[:], T.pl[r], S.pa), (S.rbk, 4, T.rb[:], T.bl[r], S.baf)]
-    jobs += [(S["rk%d" % k], 2, _buf(T, "ro", k, d)[:], _buf(T, "ol", k, d)[r], S["oa%d" % k]) for k in range(NR)]
-    if d >= TOP - 1:
-        jobs.insert(len(jobs) - 1, (S.rsa, n_in - ne, T.rfa[:], T.fla[r], S.faa))
-    if d == TOP:
-        jobs.append((S.rsb, n_in, T.rfb[:], T.flb[r], S.fab))
+
+    def n_in(ds):
+        return len(_deal(T, topo, near, far, r, ds)[d])
+
+    jobs = [(S.rp, n_in(range(N)), T.pst[:], T.pl[r], S.pa)]
+    jobs += [(S["rw%d" % k], n_in(range(N)), _wbuf(T, k, r)[0], _wbuf(T, k, r)[N + r], S["wa%d" % k])
+             for k in range(NWR) if _words(k, r)[1]]
+    jobs += [(S["rk%d" % k], n_in(_dests(k)), _obuf(T, k, d)[0], _obuf(T, k, d)[N + r], S["oa%d" % k]) for k in range(NR) if OUT[k][d]]
+    jobs += [(S["rd%d" % t], n_in(_together(t)), T["fl%d" % t][0], T["fl%d" % t][r], S["fa%d" % t]) for t in range(ND) if DIRECT[t][0] == d]
     for sem, cnt, s_ap, d_ap, rsem in jobs:
         g.wait_ge(sem, cnt)
         g.remote_dma(d_ap, s_ap, rsem, S.ls, pid, rid, m)
@@ -126,71 +168,50 @@ def rank_program(g, core, T, topo):
         for r in range(N):
             for d, h in far[r].items():
                 if h == core:
-                    relay_program(g, core, T, topo, r, d)
+                    relay_program(g, core, T, topo, near, far, r, d)
         return
     S, V, ACT, PE, SP = T.sem, g.vector, g.scalar, g.tensor, g.sync
-    me, nr, fr = rank, near[rank], sorted(far[rank])
-    e_off = topo.engines(core, T.cores[nr[0]])
-    e_all = topo.engines(core, far[me][fr[0]])
-    e_on = [e for e in e_all if e not in e_off]
-    from_far = [r for r in range(N) if me in far[r]]
-    from_near = [r for r in range(N) if me in near[r]]
-    n_far = sum(len(topo.engines(far[r][me], core)) for r in from_far)
-    n_near = sum(len(topo.engines(T.cores[r], core)) for r in from_near)
+    me = rank
     row0 = min(5 * me, 24)
     o = 5 * me - row0
     ls = [0]
 
-    def send(dests, near_es, far_es, src_of, near_dst, near_sem, far_dst, far_sem):
-        tr = []
+    def send(dests, among, src_of, near_dst, near_sem, far_dst, far_sem):
+        es, tr = _deal(T, topo, near, far, me, among), []
         for d in dests:
-            if d in nr:
-                es = near_es(d)
-                tr.append(_xfer(topo, core, T.cores[d], es, near_sem, src_of(d), near_dst))
-            elif d in fr:
-                es = far_es(d)
-                tr.append(_xfer(topo, core, far[me][d], es, far_sem, src_of(d), far_dst))
+            if d in near[me]:
+                tr.append(_xfer(topo, core, T.cores[d], es[d], near_sem, src_of(d), near_dst))
+            elif d in far[me]:
+                tr.append(_xfer(topo, core, far[me][d], es[d], far_sem, src_of(d), far_dst))
             else:
                 continue
-            ls[0] += len(es)
+            ls[0] += len(es[d])
         if tr:
             g.remote_dma_fused(tr, local_sem=S.ls)
 
-    def two_off(d):
-        return e_off[2 * nr.index(d):2 * nr.index(d) + 2]
+    def arrivals(senders, among):
+        return sum(len(_deal(T, topo, near, far, r, among)[me]) if me in near[r] else len(topo.engines(far[r][me], core))
+                   for r in senders if r != me)
 
-    def two_on(d):
-        return e_on[2 * fr.index(d):2 * fr.index(d) + 2]
+    def cols(s, n=1):
+        return slice(L * s, L * (s + n))
 
-    def four_all(d):
-        return e_all[4 * fr.index(d):4 * fr.index(d) + 4]
+    def ucols(s):
+        return slice(Z + L * s, Z + L * (s + 1))
 
     SP.dma_start(T.pst[0:80, :], T.par[:]).then_inc(S.pp, 16)
     ACT.dma_start(T.pst[80:128, :], T.par[:, 0:102]).then_inc(S.pp, 16)
-    qs = [SP, ACT]
-    fruns, nruns = _runs(fr), _runs(nr)
-    for i, (a, b) in enumerate(fruns):
-        qs[i % 2].dma_start(T.bst[a:b], T.book[16 * a:16 * b, :]).then_inc(S.bf, 16)
+    ACT.dma_start(T.pn[0:8, 0:F], T.par[:, 0:F]).then_inc(S.pnl, 16)
+    SP.dma_start(T.bk[0:64, :], T.book[0:64, :]).then_inc(S.bkl, 16)
+    ACT.dma_start(T.bk[64:128, :], T.book[64:128, :]).then_inc(S.bkl, 16)
     ACT.dma_start(T.pl[me, 0:80, :], T.par[:]).then_inc(S.pa, 16)
-    for i, (a, b) in enumerate(nruns):
-        qs[i % 2].dma_start(T.bst[a:b], T.book[16 * a:16 * b, :]).then_inc(S.bn, 16)
-    ACT.dma_start(T.win[16 * me:16 * me + 16, 0:ZB], T.book[16 * me:16 * me + 16, :]).then_inc(S.blo, 16)
-    nblo = 16
+    n_pa = 16 + arrivals(range(N), range(N))
 
-    fl = {"allow_small_or_imprecise_dtypes": True}
     g.iota(T.pc[:], [[16, 4]], 0, 1).then_inc(S.gi1, 1)
-    g.iota(T.m16[:], [[16, 8]], 0, 0, **fl).then_inc(S.gi1, 1)
-    g.iota(T.ee[:], [[1, 128]], 0, -1, **fl).then_inc(S.gi2, 1)
-    g.iota(T.rr[:], [[1, 8], [0, 16]], 0, 0, **fl).then_inc(S.gi2, 1)
-    g.iota(T.qq[:], [[0, 8], [1, 16]], 0, 0, **fl).then_inc(S.gi2, 1)
+    g.iota(T.jj[:], [[1, 136]], 0, 0).then_inc(S.gi1, 1)
+    g.iota(T.crow2[0:1, 0:6 * F], [[0, F], [16, 6]], 0, 0, allow_small_or_imprecise_dtypes=True).then_inc(S.gi2, 1)
     g.wait_ge(S.pp, 32)
-    send(range(N), two_off, two_on, lambda d: T.pst[:], T.pl[me], S.pa, T.pst[:], S.rp)
-    g.wait_ge(S.bf, 16 * len(fruns))
-    send(fr, None, four_all, lambda d: T.bst[d], None, None, T.rb[:], S.rbk)
-    g.wait_ge(S.bn, 16 * len(nruns))
-    send(nr, two_off, None, lambda d: T.bst[d], T.bl[me], S.ban, None, None)
-    g.iota(T.zz[:, 0:136], [[1, 136]], SELA, -4, **fl).then_inc(S.gi3, 1)
-    g.iota(T.zz[:, 136:272], [[1, 136]], SELB, -8, **fl).then_inc(S.gi3, 1)
+    send(range(N), range(N), lambda d: T.pst[:], T.pl[me], S.pa, T.pst[:], S.rp)
 
     vs = [0]
 
@@ -211,239 +232,313 @@ def rank_program(g, core, T, topo):
     def c(j):
         return T.col[:, j:j + 1]
 
-    RF, RM1, RC, MQ, C1O, C2O, C1L, C2L, N16, N96, SUB = range(11)
-    V.memset(T.win[:, ZB:ZB + ZP], 0.0).then_inc(S.z0, 1)
+    PF, P16, QF, RF, RM1, RC, MQ0, MQ1, C1O, C2O, C1L, C2L, SUB, BIAS, SEL = range(15)
+    p_i, qi, ri = T.pc[:, 0:1], T.ci[:, 0:1], T.ci[:, 1:2]
+    inc(V.memset(T.onesb[0:1, :], 1.0))
     inc(V.memset(T.ones[0:1, :], 1.0))
+    inc(V.memset(T.ps[:], MID))
+    inc(V.memset(T.uu[:, 0:Z], 0))
     V.wait_ge(S.gi1, 2)
-    qi, ri = T.ci[:, 0:1], T.ci[:, 1:2]
-    ts(qi, T.pc[:, 0:1], 15, A.bitwise_and)
-    ts(ri, T.pc[:, 0:1], 4, A.arith_shift_right)
+    ts(T.rr[:], T.jj[:, 0:128], 4, A.arith_shift_right)
+    ts(c(PF), p_i, 0.0, A.add)
+    ts(qi, p_i, 15, A.bitwise_and)
+    ts(ri, p_i, 4, A.arith_shift_right)
     phase()
-    ts(c(RF), ri, 0.0, A.add)
-    ts(c(RM1), ri, -1.0, A.add)
-    ts(c(RC), ri, float(16 + SKEW), A.mult, float(LEAD - 4), A.add)
-    ts(c(MQ), qi, -1.0, A.mult, MAGIC, A.add)
+    ts(T.sel96[0:8, :], T.rr[0:8, :], T.col[0:8, PF:PF + 1], A.is_equal, float(L), A.mult)
+    ts(c(QF), qi, 0.0, A.add)
     ts(c(C1O), qi, float(o + 2), A.is_equal, -1.0 / 32, A.mult)
     ts(c(C2O), qi, float(o + 1), A.is_equal, -1.0, A.mult)
     ts(c(C1L), qi, float(o + 4), A.is_equal, -1.0 / 32, A.mult)
     ts(c(C2L), qi, float(o + 3), A.is_equal, -1.0, A.mult)
-    ts(c(N16), qi, float(o), A.is_equal, float(NW), A.mult)
-    ts(c(N96), qi, float(o), A.is_equal, float(L), A.mult)
+    ts(c(RF), ri, 0.0, A.add)
+    ts(c(RM1), ri, -1.0, A.add)
+    ts(c(RC), ri, float(16 + K), A.mult, -4.0, A.add)
+    v_w = vs[0]
+    V.wait_ge(S.pnl, 16)
+    V.tensor_copy(T.nb16[0:8, 0:F], T.pn[0:8, 0:F]).then_inc(S.nbs, 1)
     phase()
-    V.wait_ge(S.gi2, 3)
-    cols = []
-    for k, (eng, crit, u0, u1) in enumerate(OPS):
-        b, c0 = PLACE[k]
-        for u in range(u0, u1):
-            cols.append((u // 6, u % 6, (0, OFF_LOW, OFF_B)[u // 6], b, c0 + u - u0, u1 - u0))
-    for li, m, ahead, b, c0, w in cols:
-        base = 16 * m + 31.0 / 64
-        if li < 2:
-            base += (XB if li else UB) - MID + L * (ahead - LEAD - SKEW * li)
-        c1 = 512 * b + c0
-        ts(T.crow[0:1, c1:c1 + w * (NE - 1) + 1:w], T.ee[0:1, 0:NE], float(L if li < 2 else 0), A.mult, base, A.add)
+    ts(T.qq[:], T.jj[:, 0:128], 15, A.bitwise_and)
+    ts(c(MQ0), qi, -1.0, A.mult, MAGIC, A.add)
+    ts(c(MQ1), qi, -1.0, A.mult, MAGIC + L * K, A.add)
+    ts(c(P16), p_i, 16.0, A.add)
+    ts(c(BIAS), p_i, 16.0, A.is_ge, 128.0 * KK, A.mult)
     ts(c(SUB), c(C2O), c(C2L), A.add, float(-MID), A.mult)
+
+    mine = [k for k in range(NWR) if _words(k, me)[1]]
+    PE.wait_ge(S.vs, v_w)
+    PE.wait_ge(S.gi2, 1)
+    PE.matmul(T.pw[:, 0:6 * F], T.onesb[0:1, :], T.crow2[0:1, 0:6 * F], True, False)
+    PE.wait_ge(S.nbs, 1)
+    for m in range(6):
+        ins = PE.matmul(T.pw[:, m:6 * F:6], T.sel96[0:8, :], T.nb16[0:8, 0:F], False, m == 5)
+    ins.then_inc(S.pwf, 1)
+    c1 = 6 * _words(mine[0], me)[1]
+    V.wait_ge(S.pwf, 1)
+    V.tensor_scalar(T.woff[:, 0:c1], T.pw[:, 0:c1], c(QF), None, A.add).then_inc(S.wo1, 1)
+    V.tensor_scalar(T.woff[:, c1:6 * F], T.pw[:, c1:6 * F], c(QF), None, A.add).then_inc(S.wo2, 1)
+
+    for m in range(6):
+        ts(T.crow[0:1, m:6 * NSTEP:6], T.jj[0:1, 0:NSTEP], float(L), A.mult, Z + 16 * m + 31.0 / 64 - MID, A.add)
     ts(T.tt[:], T.pc[:], c(RC), A.subtract)
-    ts(T.cm[:, 0:8], T.m16[:], c(C1O), A.mult)
-    ts(T.cm[:, 8:16], T.m16[:], c(C1L), A.mult)
-    ts(T.y0[:, 0:128], T.qq[:], c(C1O), A.mult, c(C2O), A.add)
-    ts(T.y0[:, 128:256], T.qq[:], c(C1L), A.mult, c(C2L), A.add)
+    ts(T.cm[:, 0:8], T.jj[:, 0:128:16], c(C1O), A.mult)
+    ts(T.cm[:, 8:16], T.jj[:, 0:128:16], c(C1L), A.mult)
     ts(T.nb[:, 0:128], T.rr[:], c(RF), A.not_equal, 1024.0, A.mult)
     ts(T.nb[:, 128:256], T.rr[:], c(RM1), A.not_equal, 1024.0, A.mult)
+    for j in range(2):
+        ts(c(SEL + j), p_i, 8.0, A.mult, 8.0 - 128.0 * (TOP - 1 + j), A.add)
     v_crow = phase()
-    V.wait_ge(S.z0, 1)
+    ts(T.y0[:, 0:128], T.qq[:], c(C1O), A.mult, c(C2O), A.add)
+    ts(T.y0[:, 128:256], T.qq[:], c(C1L), A.mult, c(C2L), A.add)
     ts(T.sk[:], T.tt[:], 3.0, A.max, 38.0, A.min)
-    ts(T.ps[:], T.win[:, ZB:ZB + 40], c(N16), A.add, c(SUB), A.add)
-    inc(V.tensor_tensor(T.uu[:], T.y0[:], T.nb[:], A.add))
-    v_ps = phase()
+    ts(T.ident[:], T.jj[:, 0:128], c(PF), A.is_equal)
+    ts(T.shift[:], T.jj[:, 0:128], c(P16), A.is_equal, -1.0, A.mult)
+    phase()
+    inc(V.tensor_tensor(T.wu[:], T.y0[:], T.nb[:], A.add))
+    for j in range(2):
+        ts(T.sel[:, 136 * j:136 * j + 136], T.jj[:], c(SEL + j), A.is_equal)
+    phase()
     for li in range(2):
         for m in range(6):
             j = 6 * li + m
-            ts(T.wt[:, 128 * j:128 * j + 128], T.uu[:, 128 * li:128 * li + 128], T.cm[:, 8 * li + m:8 * li + m + 1], A.add, 0.0, A.min)
-    ts(T.wt[:, 128 * 12:128 * 13], T.rr[:], c(RF), A.is_equal, c(N96), A.mult)
-    ts(T.ident[:], T.ee[:], 0.0, A.is_equal)
-    ts(T.shift[:], T.ee[:], 16.0, A.is_equal, -1.0, A.mult)
-    V.wait_ge(S.gi3, 2)
-    ts(T.sel[:], T.zz[:], 0.0, A.is_equal)
-    inc(V.memset(T.uw[:, 2 * ZP:4 * ZP], 0.0))
-    v_all = phase()
+            ts(T.wt[:, 128 * j:128 * j + 128], T.wu[:, 128 * li:128 * li + 128], T.cm[:, 8 * li + m:8 * li + m + 1], A.add, 0.0, A.min)
+    v_all = vs[0]
 
-    ACT.wait_ge(S.z0, 1)
-    for j in range(1, 4):
-        ACT.activation(T.win[:, ZB + j * ZP:ZB + (j + 1) * ZP], T.win[:, ZB:ZB + ZP], AF.Copy).then_inc(S.z1, 1)
-    for j in range(2):
-        ACT.activation(T.uw[:, j * ZP:(j + 1) * ZP], T.win[:, ZB:ZB + ZP], AF.Copy).then_inc(S.z1, 1)
+    nwl = [0] * NWR
+    ngd = [0] * NWR
 
-    SP.wait_ge(S.vs, v_ps)
-    SP.wait_ge(S.pa, 16 + 2 * len(from_near) + n_far)
+    def stage(q, k):
+        f0, n = _words(k, me)
+        q.wait_ge(S["wgd%d" % k], ngd[k])
+        q.dma_start(_wbuf(T, k, me)[0:N], T.wg[:, cols(f0, n)]).then_inc(S["wsd%d" % k], 16)
+        q.dma_start(T.wd[16 * me:16 * me + 16, cols(f0 + K * me, n)], T.wg[16 * me:16 * me + 16, cols(f0, n)]).then_inc(S["wl%d" % k], 16)
+        nwl[k] += 16
+
+    ACT.wait_ge(S.bkl, 32)
+    ACT.wait_ge(S.wo1, 1)
+    V.wait_ge(S.bkl, 32)
+    V.wait_ge(S.wo2, 1)
+    late = []
+    for k in mine:
+        f0, n = _words(k, me)
+        cut = min(max(F - VF, f0), f0 + n)
+        if k == mine[1]:
+            ACT.wait_ge(S.wo2, 1)
+        if cut > f0:
+            ACT.activation(T.wg[:, cols(f0, cut - f0)], T.bk[:].indirect(T.woff[:, 6 * f0:6 * cut]), AF.Copy).then_inc(S["wgd%d" % k], 1)
+            ngd[k] += 1
+        if cut < f0 + n:
+            V.tensor_copy(T.wg[:, cols(cut, f0 + n - cut)], T.bk[:].indirect(T.woff[:, 6 * cut:6 * (f0 + n)])).then_inc(S["wgd%d" % k], 1)
+            ngd[k] += 1
+            late.append(k)
+        else:
+            stage(SP if k == mine[0] else ACT, k)
+    for k in mine:
+        if k == 2:
+            g.wait_ge(S.pa, n_pa)
+        if WGO[k]:
+            g.wait_ge(S.us, WGO[k])
+        g.wait_ge(S["wsd%d" % k], 16)
+        send(range(N), range(N), lambda d: _wbuf(T, k, me)[d], _wbuf(T, k, me)[N + me], S["wa%d" % k], _wbuf(T, k, me)[0], S["rw%d" % k])
+
+    kfill = max(k for k in range(NWR) if WB[k] <= F)
+    for r in range(TOP):
+        n = NSTEP - F - K * r
+        SP.dma_start(T.wd[16 * r:16 * r + 16, cols(F + K * r, n)], T.book[0:n, :]).then_inc(S["wl%d" % kfill], 16)
+        nwl[kfill] += 16
+
+    def land(k):
+        senders = [r for r in range(N) if r != me and _words(k, r)[1]]
+        if senders:
+            SP.wait_ge(S["wa%d" % k], arrivals(senders, range(N)))
+        for s0, n in sorted(set((_words(k, r)[0] + K * r, _words(k, r)[1]) for r in senders)):
+            for a, b in _runs([r for r in senders if (_words(k, r)[0] + K * r, _words(k, r)[1]) == (s0, n)]):
+                SP.dma_start(T.wd[16 * a:16 * b, cols(s0, n)], _wbuf(T, k, a)[N + a:N + b]).then_inc(S["wl%d" % k], 16)
+                nwl[k] += 16
+
+    SP.wait_ge(S.vs, v_w)
+    SP.wait_ge(S.pa, n_pa)
     SP.dma_start(T.ps[:, 4:38], T.pl[:, 2 * row0:2 * row0 + 32, :]).then_inc(S.plo, 16)
-    ACT.wait_ge(S.ban, 2 * len(from_near))
-    for a, b in _runs(from_near):
-        ACT.dma_start(T.win[16 * a:16 * b, 0:ZB], T.bl[a:b]).then_inc(S.blo, 16)
-        nblo += 16
-    ACT.wait_ge(S.baf, n_far)
-    SP.wait_ge(S.baf, n_far)
-    for i, (a, b) in enumerate(_runs(from_far)):
-        [SP, ACT][i % 2].dma_start(T.win[16 * a:16 * b, 0:ZB], T.bl[a:b]).then_inc(S.blo, 16)
-        nblo += 16
+    land(0)
+    land(1)
+    for k in late:
+        stage(SP, k)
 
-    po = [T.po0, T.po1, T.po2]
+    po = [T.po0, T.po1]
     PE.wait_ge(S.vs, v_crow)
-    for b in range(3):
-        PE.matmul(po[b][:, 0:FILL[b]], T.ones[0:1, :], T.crow[0:1, 512 * b:512 * b + FILL[b]], True, False)
+    for b in range(2):
+        PE.matmul(po[b][:, 0:6 * NSTEP], T.ones[0:1, :], T.crow[0:1, 0:6 * NSTEP], True, False)
+    V.wait_ge(S.vs, v_all)
     V.wait_ge(S.plo, 16)
     V.tensor_scalar(T.rm[:], T.ps[:, 0:40].indirect(T.sk[:, 0:4]), c(SUB), None, A.subtract).then_inc(S.rg, 1)
     PE.wait_ge(S.vs, v_all)
     PE.wait_ge(S.rg, 1)
-    for b in range(3):
-        mine = [x for x in cols if x[3] == b]
-        for i, (li, m, ahead, _b, c0, w) in enumerate(mine):
-            j = 12 if li == 2 else 6 * li + m
-            ins = PE.matmul(po[b][:, c0:c0 + w * (NE - 1) + 1:w], T.wt[:, 128 * j:128 * j + 128], T.rm[:, ahead:ahead + NE],
-                            False, i == len(mine) - 1)
+    for b in range(2):
+        for m in range(6):
+            j = 6 * b + m
+            ins = PE.matmul(po[b][:, m:6 * NSTEP:6], T.wt[:, 128 * j:128 * j + 128], T.rm[:, 0:NSTEP], False, m == 5)
         ins.then_inc(S["pf%d" % b], 1)
-    for b in range(3):
-        V.wait_ge(S["pf%d" % b], 1)
-        V.tensor_scalar(T.off[:, 512 * b:512 * b + FILL[b]], po[b][:, 0:FILL[b]], MAGIC, c(MQ), A.add, A.subtract).then_inc(S["of%d" % b], 1)
 
-    Q = {"D": V, "A": ACT}
-    seen = {"D": [], "A": []}
-    for q in (V, ACT):
-        q.wait_ge(S.z1, 5)
-    ACT.wait_ge(S.blo, nblo)
-    cnt = {}
+    def rounded(b, s0, s1, sem):
+        V.tensor_scalar(T.off[:, LOW * b + 6 * s0:LOW * b + 6 * s1], po[b][:, 6 * s0:6 * s1], MAGIC, c(MQ1 if b else MQ0),
+                        A.add, A.subtract).then_inc(sem, 1)
 
-    def needed(k, e):
-        eng, crit, u0, u1 = OPS[k]
-        return any(0 <= e + (0, OFF_LOW, OFF_B)[u // 6] < NSTEP for u in range(u0, u1))
+    half = (FIRST + NSTEP) // 2
+    rest = {1: (0, FIRST, half), 2: (1, FIRST, half), 3: (0, half, NSTEP), 4: (1, half, NSTEP)}
+    V.wait_ge(S.pf0, 1)
+    rounded(0, 0, FIRST, S.of0a)
+    V.wait_ge(S.pf1, 1)
+    rounded(1, 0, FIRST, S.of1a)
 
-    def gather(k, e):
-        eng, crit, u0, u1 = OPS[k]
-        b, c0 = PLACE[k]
-        if b not in seen[eng]:
-            Q[eng].wait_ge(S["of%d" % b], 1)
-            seen[eng].append(b)
-        w, t = u1 - u0, e + LEAD
-        src = (T.uw[:, 0:UB + L * e] if crit else T.win[:, 0:XB + L * max(e, 0)]).indirect(
-            T.off[:, 512 * b + c0 + w * t:512 * b + c0 + w * (t + 1)])
-        out = T.gat[:, 288 * t + 16 * u0:288 * t + 16 * u1]
-        ins = V.tensor_scalar(out, src, 127.0, -127.0, A.min, A.max) if eng == "D" else ACT.activation(out, src, AF.Copy)
-        name = "g%d_%d" % (k, t % 3)
-        ins.then_inc(S[name], 1)
-        cnt[name] = cnt.get(name, 0) + 1
-        cnt[(k, e)] = (name, cnt[name])
+    def turn(name, s, first=0):
+        return S["%s%d" % (name, s % K)], len([x for x in range(first, s + 1) if x % K == s % K])
 
-    waited = {}
+    def px(s):
+        return T["px%d" % (s % NPX)][:, 0:L]
 
-    def wait_x(q, done, both=True):
-        for s in range(max(done - 2, 0) if both else done - 1, done):
-            q.wait_ge(S["cl%d" % (s % 2)], s // 2 + 1)
+    vx = {0: 0}
+    V.wait_ge(*turn("pe", 0))
+    V.tensor_scalar(T.uu[:, ucols(0)], px(0), KK, None, A.mult).then_inc(S.us, 1)
+    V.wait_ge(S.of0a, 1)
+    for e in range(1, NSTEP + 1):
+        V.wait_ge(S.us, e)
+        if e < NSTEP:
+            if e == FIRST:
+                V.wait_ge(S.of0b, 2)
+            V.wait_ge(*turn("cp", e, 1))
+            V.tensor_tensor(T.uu[:, ucols(e)], T.uu[:, 0:Z + L * e].indirect(T.off[:, 6 * e:6 * e + 6]), T.cc[:, cols(e)],
+                            A.add).then_inc(S.us, 1)
+        if e in rest:
+            rounded(*rest[e], S["of%db" % rest[e][0]])
+        vx[e] = vx[e - 1]
+        if vx[e]:
+            V.wait_ge(S.vx, vx[e])
+        V.tensor_scalar(T.xw[:, cols(e - 1)], T.uu[:, ucols(e - 1)], 1.0 / KK, 128.0, A.mult, A.add).then_inc(S.vx, 1)
+        vx[e] += 1
+        if 0 <= e - 2 < LAST_SLOT:
+            V.tensor_scalar(T.xx[:, cols(e - 2)], T.xw[:, cols(e - 2)], -128.0, None, A.add).then_inc(S.vx, 1)
+            vx[e] += 1
 
-    def bound(s):
-        V.tensor_scalar(T.win[:, XB + L * s:XB + L * s + L], T.uw[:, UB + L * s:UB + L * s + L], 127.0, -127.0,
-                        A.min, A.max).then_inc(S["cl%d" % (s % 2)], 1)
+    def lower(s):
+        if s == FIRST:
+            ACT.wait_ge(S.of1b, 2)
+        ACT.wait_ge(S.us, s - K + 1)
+        ACT.activation(T.lg[:, cols(s)], T.uu[:, 0:Z + L * (s - K + 1)].indirect(T.off[:, LOW + 6 * s:LOW + 6 * s + 6]), AF.Identity,
+                       bias=128.0, scale=1.0 / KK).then_inc(turn("gl", s, K)[0], 1)
 
-    def sum_in(s, li, first, last):
-        e = s - (0, OFF_LOW, OFF_B)[li]
-        for k, (eng, crit, u0, u1) in enumerate(OPS):
-            if u0 < 6 * li + 6 and u1 > 6 * li and (k, e) not in waited:
-                PE.wait_ge(S[cnt[(k, e)][0]], cnt[(k, e)][1])
-                waited[(k, e)] = True
-        c0 = 288 * (e + LEAD) + L * li
-        return PE.matmul(T["px%d" % (s % NPX)][:, 0:L], (T.shift if li == 1 else T.ident)[:], T.gat[:, c0:c0 + L], first, last)
+    def addend(s):
+        ACT.wait_ge(*turn("pe", s))
+        ACT.activation(T.cc[:, cols(s)], px(s), AF.Identity, bias=c(BIAS) if s >= K else 0.0, scale=KK).then_inc(turn("cp", s)[0], 1)
 
-    def spread(done, parts, sel0, bank, w, sem):
-        wait_x(PE, done)
-        c0 = XB + L * (done - SKEW)
-        for j in range(parts):
-            ins = PE.matmul(bank[:, 0:w], T.sel[:, sel0 + parts - j:sel0 + parts - j + 128], T.win[:, c0 + w * j:c0 + w * (j + 1)],
-                            j == 0, j == parts - 1)
-        ins.then_inc(sem, 1)
+    for s in range(1, K):
+        addend(s)
+    ACT.wait_ge(S.of1a, 1)
+    lower(K)
+    for s in range(K, NSTEP):
+        if s + 1 < NSTEP:
+            lower(s + 1)
+        addend(s)
+    for t in range(ND):
+        w = 12 * DIRECT[t][2]
+        ACT.wait_ge(S["mm%d" % t], 1)
+        ACT.activation(T["fin%d" % t][:], T[DIRECT[t][3]][:, 0:w], AF.Identity, bias=-128.0).then_inc(S["fc%d" % t], 1)
 
-    for e in range(-LEAD, NSTEP):
-        if e > 0:
-            V.wait_ge(S.us, e)
-            if needed(1, e):
-                wait_x(ACT, e, False)
-        for k in range(len(OPS)):
-            if needed(k, e):
-                gather(k, e)
-        if e > 0:
-            bound(e - 1)
-        if e == NSTEP - SKEW + 1:
-            V.wait_ge(S.mma, 1)
-            V.tensor_copy(T.fina[:], T.po1[:, 0:WA]).then_inc(S.cpa, 1)
-        if 0 <= e + 1 < NSTEP:
-            sum_in(e + 1, 2, True, False)
-            if e == NSTEP - SKEW:
-                spread(e, 4, 0, T.po1, WA, S.mma)
-            sum_in(e + 1, 1, False, True).then_inc(S["pe%d" % ((e + 1) % 2)], 1)
-        if e >= 0:
-            V.wait_ge(S[cnt[(0, e)][0]], cnt[(0, e)][1])
-            V.wait_ge(S["pe%d" % (e % 2)], e // 2 + 1)
-            c0 = 288 * (e + LEAD)
-            V.tensor_tensor(T.uw[:, UB + L * e:UB + L * e + L], T.gat[:, c0:c0 + L], T["px%d" % (e % NPX)][:, 0:L], A.add).then_inc(S.us, 1)
-    V.wait_ge(S.us, NSTEP)
-    bound(NSTEP - 1)
-    spread(NSTEP, 8, 136, T.po0, WB, S.mmb)
-    V.wait_ge(S.mmb, 1)
-    V.tensor_copy(T.finb[:], T.po0[:, 0:WB]).then_inc(S.cpb, 1)
-
-    jobs = sorted((sum(_frames(k, r)) + SKEW * r, k, r) for k in range(NR) for r in range(N))
+    jobs = sorted([(sum(_frames(k, r)) + K * r, 0, k, r) for k in range(NR) for r in _dests(k)]
+                  + [(WLAND[k], 1, k, 0) for k in range(2, NWR)])
     last = 0
-    for done, k, r in jobs:
+    for done, kind, k, r in jobs:
+        if kind:
+            land(k)
+            continue
         if done > last:
-            wait_x(SP, done)
+            SP.wait_ge(S.vx, vx[done + 1])
             last = done
         f0, n = _frames(k, r)
-        c0 = XB + L * (f0 + SKEW * r)
-        out = _buf(T, "ol", k, r)[me] if r == me else _buf(T, "ost", k, r)[r]
-        SP.dma_start(out, T.win[16 * r:16 * r + 16, c0:c0 + L * n]).then_inc(S["so%d" % k], 16)
+        SP.dma_start(_obuf(T, k, r)[N + me if r == me else r], T.xx[16 * r:16 * r + 16, cols(f0 + K * r, n)]).then_inc(S["so%d" % k], 16)
+
+    def spread(st):
+        PE.wait_ge(S.vx, vx[st + 1])
+        for t, (r, s0, n, bank) in enumerate(DIRECT):
+            w = 12 * n
+            for j in range(8):
+                if s0 + (w * (j + 1) - 1) // L == st:
+                    if j == 0:
+                        for t0 in range(t):
+                            if DIRECT[t0][3] == bank:
+                                PE.wait_ge(S["fc%d" % t0], 1)
+                    s1 = 136 * (r - TOP + 1) + 8 - j
+                    ins = PE.matmul(T[bank][:, 0:w], T.sel[:, s1:s1 + 128], T.xw[:, L * s0 + w * j:L * s0 + w * (j + 1)], j == 0, j == 7)
+                    if j == 7:
+                        ins.then_inc(S["mm%d" % t], 1)
+
+    for s in range(NSTEP + K):
+        if s < NSTEP:
+            if s in WB:
+                PE.wait_ge(S["wl%d" % WB.index(s)], nwl[WB.index(s)])
+            p = 16 * min(N, s // K + 1)
+            ins = PE.matmul(px(s), T.ident[0:p, :], T.wd[0:p, cols(s)], True, s < K)
+            if s >= K:
+                PE.wait_ge(*turn("gl", s, K))
+                ins = PE.matmul(px(s), T.shift[:], T.lg[:, cols(s)], False, True)
+            ins.then_inc(turn("pe", s)[0], 1)
+        if s - K >= DIRECT[0][1]:
+            spread(s - K)
 
     def round_out(k):
-        g.wait_ge(S["so%d" % k], 16 * N)
-        for n in sorted(set(_frames(k, r)[1] for r in range(N))):
-            ds = [r for r in range(N) if _frames(k, r)[1] == n]
-            send(ds, two_off, two_on, lambda d: _buf(T, "ost", k, d)[d], _buf(T, "ol", k, ds[0])[me], S["oa%d" % k],
-                 _buf(T, "ro", k, ds[0])[:], S["rk%d" % k])
+        g.wait_ge(S["so%d" % k], 16 * len(_dests(k)))
+        for n in sorted(set(OUT[k]) - {0}):
+            ds = [r for r in range(N) if OUT[k][r] == n]
+            buf = _obuf(T, k, ds[0])
+            send(ds, _dests(k), lambda d: buf[d], buf[N + me], S["oa%d" % k], buf[0], S["rk%d" % k])
+
+    nst = [0, 0]
 
     def store(k):
         f0, n = _frames(k, me)
-        g.wait_ge(S["oa%d" % k], 2 * len(from_near) + n_far)
-        g.dma_start(T.y[:, L * f0:L * (f0 + n)], _buf(T, "ol", k, me)[:]).then_inc(S.st, 16)
+        if n:
+            g.wait_ge(S["oa%d" % k], arrivals(range(N), _dests(k)))
+            g.dma_start(T.y[:, cols(f0, n)], _obuf(T, k, me)[N:2 * N]).then_inc(S.st, 16)
+            nst[0] += 16
+
+    def direct(ts_):
+        tr = []
+        for t in ts_:
+            r = DIRECT[t][0]
+            if r == me:
+                continue
+            es = _deal(T, topo, near, far, me, _together(t))[r]
+            g.wait_ge(S["fc%d" % t], 1)
+            if r in near[me]:
+                tr.append(_xfer(topo, core, T.cores[r], es, S["fa%d" % t], T["fin%d" % t][:], T["fl%d" % t][me]))
+            else:
+                tr.append(_xfer(topo, core, far[me][r], es, S["rd%d" % t], T["fin%d" % t][:], T["fl%d" % t][0]))
+            ls[0] += len(es)
+        if tr:
+            g.remote_dma_fused(tr, local_sem=S.ls)
 
     round_out(0)
     round_out(1)
     store(0)
-    for k in range(2, NR - 1):
-        round_out(k)
-    g.wait_ge(S.cpa, 1)
-    send([TOP - 1, TOP], lambda d: e_off, lambda d: e_on, lambda d: T.fina[:], T.fla[me], S.faa, T.rfa[:], S.rsa)
-    round_out(NR - 1)
-    if me != TOP:
-        g.wait_ge(S.cpb, 1)
-        send([TOP], lambda d: e_off, lambda d: e_all, lambda d: T.finb[:], T.flb[me], S.fab, T.rfb[:], S.rsb)
-    for k in range(1, NR):
+    round_out(2)
+    store(1)
+    round_out(3)
+    round_out(4)
+    direct([0, 1])
+    direct([2])
+    direct([3])
+    for k in range(2, NR):
         store(k)
     g.wait_ge(S.ls, ls[0])
-    g.wait_ge(S.st, 16 * NR)
+    g.wait_ge(S.st, nst[0])
 
-    nst = [0]
-
-    def final(cp, fin, land, sem, p0, p1, f0):
-        t0, t1 = L * f0, L * (f0 + SKEW)
-        SP.wait_ge(cp, 1)
-        SP.dma_start(T.y[16 * me:16 * me + 16, t0:t1], fin[p0:p1, :]).then_inc(S.stf, 16)
-        SP.wait_ge(sem, n_near + n_far)
-        runs = _runs([r for r in range(N) if r != me])
-        for a, b in runs:
-            SP.dma_start(T.y[16 * a:16 * b, t0:t1], land[a:b, p0:p1, :]).then_inc(S.stf, 16)
-        nst[0] += 16 * (1 + len(runs))
-
-    if me == TOP - 1:
-        final(S.cpa, T.fina, T.fla, S.faa, 0, 64, F - SKEW)
-    if me == TOP:
-        final(S.cpa, T.fina, T.fla, S.faa, 64, 128, F - 2 * SKEW)
-        final(S.cpb, T.finb, T.flb, S.fab, 0, 128, F - SKEW)
-    if nst[0]:
-        SP.wait_ge(S.stf, nst[0])
+    for t, (r, s0, n, bank) in enumerate(DIRECT):
+        if r == me:
+            tc = cols(s0 - K * r, n)
+            SP.wait_ge(S["fc%d" % t], 1)
+            SP.dma_start(T.y[16 * me:16 * me + 16, tc], T["fin%d" % t][:]).then_inc(S.stf, 16)
+            SP.wait_ge(S["fa%d" % t], arrivals(range(N), _together(t)))
+            runs = _runs([x for x in range(N) if x != me])
+            for a, b in runs:
+                SP.dma_start(T.y[16 * a:16 * b, tc], T["fl%d" % t][a:b]).then_inc(S.stf, 16)
+            nst[1] += 16 * (1 + len(runs))
+    if nst[1]:
+        SP.wait_ge(S.stf, nst[1])

from concourse.bass import DstId, RemoteDMATransfer
from concourse.mybir import AluOpType as A, ActivationFunctionType as AF

N, F, L, NW = 8, 34, 96, 16
K = 4
NSTEP = F + K * (N - 1)
TOP = N - 1
Z = 16
KK = float(2 ** 24 + 2 ** 17 + 2 ** 10)
MID = 1632
MAGIC = 12582912.0
NPX = K + 1
LOW = 384
FIRST = 16

WB = [0, 4, 12, 24, 40, NSTEP]
WGO = [0, 0, 0, 2, 14]
WLAND = [0, 0, 0, 0, 26]
VF = 8
OUT = [[12, 12, 12, 6, 6, 0, 0, 0], [12, 12, 12, 12, 12, 14, 10, 6], [10] * 8, [0, 0, 0, 6, 6, 6, 6, 6], [0, 0, 0, 0, 0, 4, 4, 4]]
DIRECT = [(6, 54, 4, "po0"), (7, 54, 4, "po1"), (7, 58, 2, "pw"), (7, 60, 2, "po0")]
NWR, NR, ND = len(WB) - 1, len(OUT), len(DIRECT)
LAST_SLOT = max(K * r + sum(o[r] for o in OUT) for r in range(N))


def _words(k, r):
    f0, f1 = min(max(WB[k] - K * r, 0), F), min(max(WB[k + 1] - K * r, 0), F)
    return f0, f1 - f0


def _frames(k, r):
    return sum(o[r] for o in OUT[:k]), OUT[k][r]


SCRATCH = {
    "pst": ("dram", [128, 17], "int32"), "pl": ("dram", [N, 128, 17], "int32"),
    "bk": ("sbuf", [128, NW * L], "bfloat16"), "wg": ("sbuf", [128, F * L], "bfloat16"),
    "pn": ("sbuf", [128, 40], "int32"), "nb16": ("sbuf", [128, 40], "bfloat16"), "woff": ("sbuf", [128, 208], "uint16"),
    "crow2": ("sbuf", [128, 208], "bfloat16"), "onesb": ("sbuf", [128, 128], "bfloat16"), "sel96": ("sbuf", [128, 128], "bfloat16"),
    "uu": ("sbuf", [128, Z + L * NSTEP], "int32"), "cc": ("sbuf", [128, L * NSTEP], "float32"),
    "wd": ("sbuf", [128, L * NSTEP], "bfloat16"), "lg": ("sbuf", [128, L * NSTEP], "bfloat16"),
    "xw": ("sbuf", [128, L * NSTEP], "bfloat16"), "xx": ("sbuf", [128, L * NSTEP], "bfloat16"),
    "off": ("sbuf", [128, 2 * LOW], "uint16"),
    "pc": ("sbuf", [128, 4], "int32"), "jj": ("sbuf", [128, 136], "int32"),
    "rr": ("sbuf", [128, 128], "int32"), "qq": ("sbuf", [128, 128], "int32"),
    "ci": ("sbuf", [128, 8], "int32"), "col": ("sbuf", [128, 24], "float32"), "cm": ("sbuf", [128, 16], "float32"),
    "tt": ("sbuf", [128, 4], "float32"), "sk": ("sbuf", [128, 4], "uint16"),
    "ps": ("sbuf", [128, 40], "int32"), "rm": ("sbuf", [128, 64], "float16"),
    "crow": ("sbuf", [128, LOW], "float32"), "ones": ("sbuf", [128, 128], "float32"),
    "y0": ("sbuf", [128, 256], "float32"), "nb": ("sbuf", [128, 256], "float32"), "wu": ("sbuf", [128, 256], "bfloat16"),
    "wt": ("sbuf", [128, 12 * 128], "float16"),
    "ident": ("sbuf", [128, 128], "bfloat16"), "shift": ("sbuf", [128, 128], "bfloat16"),
    "sel": ("sbuf", [128, 2 * 136], "bfloat16"),
    "po0": ("psum", [128, 512], "float32"), "po1": ("psum", [128, 512], "float32"), "pw": ("psum", [128, 512], "float32"),
}
for _k in range(NPX):
    SCRATCH["px%d" % _k] = ("psum", [128, 512], "float32")
for _r in range(N):
    for _k in range(NWR):
        if _words(_k, _r)[1]:
            SCRATCH["ws%d_%d" % (_k, _words(_k, _r)[1])] = ("dram", [2 * N, 128, 12 * _words(_k, _r)[1]], "bfloat16")
    for _k in range(NR):
        if OUT[_k][_r]:
            SCRATCH["os%d_%d" % (_k, OUT[_k][_r])] = ("dram", [2 * N, 128, 12 * OUT[_k][_r]], "bfloat16")
for _t in range(ND):
    SCRATCH["fin%d" % _t] = ("sbuf", [128, 12 * DIRECT[_t][2]], "float32")
    SCRATCH["fl%d" % _t] = ("dram", [N, 128, 12 * DIRECT[_t][2]], "float32")

SEMAPHORES = (["ls", "pp", "pa", "rp", "plo", "pnl", "bkl", "gi1", "gi2", "vs", "nbs", "pwf", "wo1", "wo2", "rg",
               "pf0", "pf1", "of0a", "of0b", "of1a", "of1b", "us", "vx", "st", "stf"]
              + ["%s%d" % (s, k) for s in ("gl", "pe", "cp") for k in range(K)]
              + ["%s%d" % (s, k) for s in ("wgd", "wsd", "wa", "wl", "rw") for k in range(NWR)]
              + ["%s%d" % (s, k) for s in ("so", "oa", "rk") for k in range(NR)]
              + ["%s%d" % (s, k) for s in ("mm", "fc", "rd", "fa") for k in range(ND)])


def _mask(es):
    return sum(1 << int(e) for e in es)


def _plan(T, topo):
    near, far = {}, {}
    for r, c in enumerate(T.cores):
        near[r] = [d for d in range(N) if d != r and topo.may_write(c, T.cores[d])]
        far[r] = {}
        used = []
        for d in range(N):
            if d == r or d in near[r]:
                continue
            h = [x for x in topo.cores_of(c) if x not in T.cores and topo.may_write(x, T.cores[d])]
            h.sort(key=lambda x: used.count(x))
            far[r][d] = h[0]
            used.append(h[0])
    return near, far


def _share(es, ds):
    per = 1
    while ds and 2 * per * len(ds) <= len(es):
        per *= 2
    return {d: es[per * i:per * (i + 1)] for i, d in enumerate(ds)}


def _deal(T, topo, near, far, r, ds):
    c = T.cores[r]
    e_off = topo.engines(c, T.cores[near[r][0]])
    e_all = topo.engines(c, far[r][sorted(far[r])[0]])
    dn, df = [d for d in ds if d in near[r]], [d for d in ds if d in far[r]]
    out = _share(e_off, dn)
    out.update(_share([e for e in e_all if e not in e_off] if dn else e_all, df))
    return out


def _runs(xs):
    out = []
    for x in sorted(xs):
        if out and out[-1][1] == x:
            out[-1][1] = x + 1
        else:
            out.append([x, x + 1])
    return out


def _xfer(topo, src, dst, es, sem, s_ap, d_ap):
    rid, pid = topo.addr(dst, src)
    return RemoteDMATransfer(dst_ids=[DstId(rid=rid, pnc=pid)], dma_engine_mask=_mask(es), remote_sem=sem, src=s_ap, dst=d_ap)


def _wbuf(T, k, r):
    return T["ws%d_%d" % (k, _words(k, r)[1])]


def _obuf(T, k, r):
    return T["os%d_%d" % (k, OUT[k][r])]


def _dests(k):
    return [r for r in range(N) if OUT[k][r]]


def _together(t):
    return [x[0] for x in DIRECT if x[1] + x[2] == DIRECT[t][1] + DIRECT[t][2]]


def relay_program(g, core, T, topo, near, far, r, d):
    S, dst = T.sem, T.cores[d]
    rid, pid = topo.addr(dst, core)
    m, ne = topo.mask(core, dst), len(topo.engines(core, dst))

    def n_in(ds):
        return len(_deal(T, topo, near, far, r, ds)[d])

    jobs = [(S.rp, n_in(range(N)), T.pst[:], T.pl[r], S.pa)]
    jobs += [(S["rw%d" % k], n_in(range(N)), _wbuf(T, k, r)[0], _wbuf(T, k, r)[N + r], S["wa%d" % k])
             for k in range(NWR) if _words(k, r)[1]]
    jobs += [(S["rk%d" % k], n_in(_dests(k)), _obuf(T, k, d)[0], _obuf(T, k, d)[N + r], S["oa%d" % k]) for k in range(NR) if OUT[k][d]]
    jobs += [(S["rd%d" % t], n_in(_together(t)), T["fl%d" % t][0], T["fl%d" % t][r], S["fa%d" % t]) for t in range(ND) if DIRECT[t][0] == d]
    for sem, cnt, s_ap, d_ap, rsem in jobs:
        g.wait_ge(sem, cnt)
        g.remote_dma(d_ap, s_ap, rsem, S.ls, pid, rid, m)
    g.wait_ge(S.ls, ne * len(jobs))


def rank_program(g, core, T, topo):
    near, far = _plan(T, topo)
    rank = T.rank_of(core)
    if rank is None:
        for r in range(N):
            for d, h in far[r].items():
                if h == core:
                    relay_program(g, core, T, topo, near, far, r, d)
        return
    S, V, ACT, PE, SP = T.sem, g.vector, g.scalar, g.tensor, g.sync
    me = rank
    row0 = min(5 * me, 24)
    o = 5 * me - row0
    ls = [0]

    def send(dests, among, src_of, near_dst, near_sem, far_dst, far_sem):
        es, tr = _deal(T, topo, near, far, me, among), []
        for d in dests:
            if d in near[me]:
                tr.append(_xfer(topo, core, T.cores[d], es[d], near_sem, src_of(d), near_dst))
            elif d in far[me]:
                tr.append(_xfer(topo, core, far[me][d], es[d], far_sem, src_of(d), far_dst))
            else:
                continue
            ls[0] += len(es[d])
        if tr:
            g.remote_dma_fused(tr, local_sem=S.ls)

    def arrivals(senders, among):
        return sum(len(_deal(T, topo, near, far, r, among)[me]) if me in near[r] else len(topo.engines(far[r][me], core))
                   for r in senders if r != me)

    def cols(s, n=1):
        return slice(L * s, L * (s + n))

    def ucols(s):
        return slice(Z + L * s, Z + L * (s + 1))

    SP.dma_start(T.pst[0:80, :], T.par[:]).then_inc(S.pp, 16)
    ACT.dma_start(T.pst[80:128, :], T.par[:, 0:102]).then_inc(S.pp, 16)
    ACT.dma_start(T.pn[0:8, 0:F], T.par[:, 0:F]).then_inc(S.pnl, 16)
    SP.dma_start(T.bk[0:64, :], T.book[0:64, :]).then_inc(S.bkl, 16)
    ACT.dma_start(T.bk[64:128, :], T.book[64:128, :]).then_inc(S.bkl, 16)
    ACT.dma_start(T.pl[me, 0:80, :], T.par[:]).then_inc(S.pa, 16)
    n_pa = 16 + arrivals(range(N), range(N))

    g.iota(T.pc[:], [[16, 4]], 0, 1).then_inc(S.gi1, 1)
    g.iota(T.jj[:], [[1, 136]], 0, 0).then_inc(S.gi1, 1)
    g.iota(T.crow2[0:1, 0:6 * F], [[0, F], [16, 6]], 0, 0, allow_small_or_imprecise_dtypes=True).then_inc(S.gi2, 1)
    g.wait_ge(S.pp, 32)
    send(range(N), range(N), lambda d: T.pst[:], T.pl[me], S.pa, T.pst[:], S.rp)

    vs = [0]

    def inc(ins):
        ins.then_inc(S.vs, 1)
        vs[0] += 1

    def phase():
        V.wait_ge(S.vs, vs[0])
        return vs[0]

    def ts(out, in0, s1, op0, s2=None, op1=None):
        if op1 is None:
            inc(V.tensor_scalar(out, in0, s1, None, op0))
        else:
            inc(V.tensor_scalar(out, in0, s1, s2, op0, op1))

    def c(j):
        return T.col[:, j:j + 1]

    PF, P16, QF, RF, RM1, RC, MQ0, MQ1, C1O, C2O, C1L, C2L, SUB, BIAS, SEL = range(15)
    p_i, qi, ri = T.pc[:, 0:1], T.ci[:, 0:1], T.ci[:, 1:2]
    inc(V.memset(T.onesb[0:1, :], 1.0))
    inc(V.memset(T.ones[0:1, :], 1.0))
    inc(V.memset(T.ps[:], MID))
    inc(V.memset(T.uu[:, 0:Z], 0))
    V.wait_ge(S.gi1, 2)
    ts(T.rr[:], T.jj[:, 0:128], 4, A.arith_shift_right)
    ts(c(PF), p_i, 0.0, A.add)
    ts(qi, p_i, 15, A.bitwise_and)
    ts(ri, p_i, 4, A.arith_shift_right)
    phase()
    ts(T.sel96[0:8, :], T.rr[0:8, :], T.col[0:8, PF:PF + 1], A.is_equal, float(L), A.mult)
    ts(c(QF), qi, 0.0, A.add)
    ts(c(C1O), qi, float(o + 2), A.is_equal, -1.0 / 32, A.mult)
    ts(c(C2O), qi, float(o + 1), A.is_equal, -1.0, A.mult)
    ts(c(C1L), qi, float(o + 4), A.is_equal, -1.0 / 32, A.mult)
    ts(c(C2L), qi, float(o + 3), A.is_equal, -1.0, A.mult)
    ts(c(RF), ri, 0.0, A.add)
    ts(c(RM1), ri, -1.0, A.add)
    ts(c(RC), ri, float(16 + K), A.mult, -4.0, A.add)
    v_w = vs[0]
    V.wait_ge(S.pnl, 16)
    V.tensor_copy(T.nb16[0:8, 0:F], T.pn[0:8, 0:F]).then_inc(S.nbs, 1)
    phase()
    ts(T.qq[:], T.jj[:, 0:128], 15, A.bitwise_and)
    ts(c(MQ0), qi, -1.0, A.mult, MAGIC, A.add)
    ts(c(MQ1), qi, -1.0, A.mult, MAGIC + L * K, A.add)
    ts(c(P16), p_i, 16.0, A.add)
    ts(c(BIAS), p_i, 16.0, A.is_ge, 128.0 * KK, A.mult)
    ts(c(SUB), c(C2O), c(C2L), A.add, float(-MID), A.mult)

    mine = [k for k in range(NWR) if _words(k, me)[1]]
    PE.wait_ge(S.vs, v_w)
    PE.wait_ge(S.gi2, 1)
    PE.matmul(T.pw[:, 0:6 * F], T.onesb[0:1, :], T.crow2[0:1, 0:6 * F], True, False)
    PE.wait_ge(S.nbs, 1)
    for m in range(6):
        ins = PE.matmul(T.pw[:, m:6 * F:6], T.sel96[0:8, :], T.nb16[0:8, 0:F], False, m == 5)
    ins.then_inc(S.pwf, 1)
    c1 = 6 * _words(mine[0], me)[1]
    V.wait_ge(S.pwf, 1)
    V.tensor_scalar(T.woff[:, 0:c1], T.pw[:, 0:c1], c(QF), None, A.add).then_inc(S.wo1, 1)
    V.tensor_scalar(T.woff[:, c1:6 * F], T.pw[:, c1:6 * F], c(QF), None, A.add).then_inc(S.wo2, 1)

    for m in range(6):
        ts(T.crow[0:1, m:6 * NSTEP:6], T.jj[0:1, 0:NSTEP], float(L), A.mult, Z + 16 * m + 31.0 / 64 - MID, A.add)
    ts(T.tt[:], T.pc[:], c(RC), A.subtract)
    ts(T.cm[:, 0:8], T.jj[:, 0:128:16], c(C1O), A.mult)
    ts(T.cm[:, 8:16], T.jj[:, 0:128:16], c(C1L), A.mult)
    ts(T.nb[:, 0:128], T.rr[:], c(RF), A.not_equal, 1024.0, A.mult)
    ts(T.nb[:, 128:256], T.rr[:], c(RM1), A.not_equal, 1024.0, A.mult)
    for j in range(2):
        ts(c(SEL + j), p_i, 8.0, A.mult, 8.0 - 128.0 * (TOP - 1 + j), A.add)
    v_crow = phase()
    ts(T.y0[:, 0:128], T.qq[:], c(C1O), A.mult, c(C2O), A.add)
    ts(T.y0[:, 128:256], T.qq[:], c(C1L), A.mult, c(C2L), A.add)
    ts(T.sk[:], T.tt[:], 3.0, A.max, 38.0, A.min)
    ts(T.ident[:], T.jj[:, 0:128], c(PF), A.is_equal)
    ts(T.shift[:], T.jj[:, 0:128], c(P16), A.is_equal, -1.0, A.mult)
    phase()
    inc(V.tensor_tensor(T.wu[:], T.y0[:], T.nb[:], A.add))
    for j in range(2):
        ts(T.sel[:, 136 * j:136 * j + 136], T.jj[:], c(SEL + j), A.is_equal)
    phase()
    for li in range(2):
        for m in range(6):
            j = 6 * li + m
            ts(T.wt[:, 128 * j:128 * j + 128], T.wu[:, 128 * li:128 * li + 128], T.cm[:, 8 * li + m:8 * li + m + 1], A.add, 0.0, A.min)
    v_all = vs[0]

    nwl = [0] * NWR
    ngd = [0] * NWR

    def stage(q, k):
        f0, n = _words(k, me)
        q.wait_ge(S["wgd%d" % k], ngd[k])
        q.dma_start(_wbuf(T, k, me)[0:N], T.wg[:, cols(f0, n)]).then_inc(S["wsd%d" % k], 16)
        q.dma_start(T.wd[16 * me:16 * me + 16, cols(f0 + K * me, n)], T.wg[16 * me:16 * me + 16, cols(f0, n)]).then_inc(S["wl%d" % k], 16)
        nwl[k] += 16

    ACT.wait_ge(S.bkl, 32)
    ACT.wait_ge(S.wo1, 1)
    V.wait_ge(S.bkl, 32)
    V.wait_ge(S.wo2, 1)
    late = []
    for k in mine:
        f0, n = _words(k, me)
        cut = min(max(F - VF, f0), f0 + n)
        if k == mine[1]:
            ACT.wait_ge(S.wo2, 1)
        if cut > f0:
            ACT.activation(T.wg[:, cols(f0, cut - f0)], T.bk[:].indirect(T.woff[:, 6 * f0:6 * cut]), AF.Copy).then_inc(S["wgd%d" % k], 1)
            ngd[k] += 1
        if cut < f0 + n:
            V.tensor_copy(T.wg[:, cols(cut, f0 + n - cut)], T.bk[:].indirect(T.woff[:, 6 * cut:6 * (f0 + n)])).then_inc(S["wgd%d" % k], 1)
            ngd[k] += 1
            late.append(k)
        else:
            stage(SP if k == mine[0] else ACT, k)
    for k in mine:
        if k == 2:
            g.wait_ge(S.pa, n_pa)
        if WGO[k]:
            g.wait_ge(S.us, WGO[k])
        g.wait_ge(S["wsd%d" % k], 16)
        send(range(N), range(N), lambda d: _wbuf(T, k, me)[d], _wbuf(T, k, me)[N + me], S["wa%d" % k], _wbuf(T, k, me)[0], S["rw%d" % k])

    kfill = max(k for k in range(NWR) if WB[k] <= F)
    for r in range(TOP):
        n = NSTEP - F - K * r
        SP.dma_start(T.wd[16 * r:16 * r + 16, cols(F + K * r, n)], T.book[0:n, :]).then_inc(S["wl%d" % kfill], 16)
        nwl[kfill] += 16

    def land(k):
        senders = [r for r in range(N) if r != me and _words(k, r)[1]]
        if senders:
            SP.wait_ge(S["wa%d" % k], arrivals(senders, range(N)))
        for s0, n in sorted(set((_words(k, r)[0] + K * r, _words(k, r)[1]) for r in senders)):
            for a, b in _runs([r for r in senders if (_words(k, r)[0] + K * r, _words(k, r)[1]) == (s0, n)]):
                SP.dma_start(T.wd[16 * a:16 * b, cols(s0, n)], _wbuf(T, k, a)[N + a:N + b]).then_inc(S["wl%d" % k], 16)
                nwl[k] += 16

    SP.wait_ge(S.vs, v_w)
    SP.wait_ge(S.pa, n_pa)
    SP.dma_start(T.ps[:, 4:38], T.pl[:, 2 * row0:2 * row0 + 32, :]).then_inc(S.plo, 16)
    land(0)
    land(1)
    for k in late:
        stage(SP, k)

    po = [T.po0, T.po1]
    PE.wait_ge(S.vs, v_crow)
    for b in range(2):
        PE.matmul(po[b][:, 0:6 * NSTEP], T.ones[0:1, :], T.crow[0:1, 0:6 * NSTEP], True, False)
    V.wait_ge(S.vs, v_all)
    V.wait_ge(S.plo, 16)
    V.tensor_scalar(T.rm[:], T.ps[:, 0:40].indirect(T.sk[:, 0:4]), c(SUB), None, A.subtract).then_inc(S.rg, 1)
    PE.wait_ge(S.vs, v_all)
    PE.wait_ge(S.rg, 1)
    for b in range(2):
        for m in range(6):
            j = 6 * b + m
            ins = PE.matmul(po[b][:, m:6 * NSTEP:6], T.wt[:, 128 * j:128 * j + 128], T.rm[:, 0:NSTEP], False, m == 5)
        ins.then_inc(S["pf%d" % b], 1)

    def rounded(b, s0, s1, sem):
        V.tensor_scalar(T.off[:, LOW * b + 6 * s0:LOW * b + 6 * s1], po[b][:, 6 * s0:6 * s1], MAGIC, c(MQ1 if b else MQ0),
                        A.add, A.subtract).then_inc(sem, 1)

    half = (FIRST + NSTEP) // 2
    rest = {1: (0, FIRST, half), 2: (1, FIRST, half), 3: (0, half, NSTEP), 4: (1, half, NSTEP)}
    V.wait_ge(S.pf0, 1)
    rounded(0, 0, FIRST, S.of0a)
    V.wait_ge(S.pf1, 1)
    rounded(1, 0, FIRST, S.of1a)

    def turn(name, s, first=0):
        return S["%s%d" % (name, s % K)], len([x for x in range(first, s + 1) if x % K == s % K])

    def px(s):
        return T["px%d" % (s % NPX)][:, 0:L]

    vx = {0: 0}
    V.wait_ge(*turn("pe", 0))
    V.tensor_scalar(T.uu[:, ucols(0)], px(0), KK, None, A.mult).then_inc(S.us, 1)
    V.wait_ge(S.of0a, 1)
    for e in range(1, NSTEP + 1):
        V.wait_ge(S.us, e)
        if e < NSTEP:
            if e == FIRST:
                V.wait_ge(S.of0b, 2)
            V.wait_ge(*turn("cp", e, 1))
            V.tensor_tensor(T.uu[:, ucols(e)], T.uu[:, 0:Z + L * e].indirect(T.off[:, 6 * e:6 * e + 6]), T.cc[:, cols(e)],
                            A.add).then_inc(S.us, 1)
        if e in rest:
            rounded(*rest[e], S["of%db" % rest[e][0]])
        vx[e] = vx[e - 1]
        if vx[e]:
            V.wait_ge(S.vx, vx[e])
        V.tensor_scalar(T.xw[:, cols(e - 1)], T.uu[:, ucols(e - 1)], 1.0 / KK, 128.0, A.mult, A.add).then_inc(S.vx, 1)
        vx[e] += 1
        if 0 <= e - 2 < LAST_SLOT:
            V.tensor_scalar(T.xx[:, cols(e - 2)], T.xw[:, cols(e - 2)], -128.0, None, A.add).then_inc(S.vx, 1)
            vx[e] += 1

    def lower(s):
        if s == FIRST:
            ACT.wait_ge(S.of1b, 2)
        ACT.wait_ge(S.us, s - K + 1)
        ACT.activation(T.lg[:, cols(s)], T.uu[:, 0:Z + L * (s - K + 1)].indirect(T.off[:, LOW + 6 * s:LOW + 6 * s + 6]), AF.Identity,
                       bias=128.0, scale=1.0 / KK).then_inc(turn("gl", s, K)[0], 1)

    def addend(s):
        ACT.wait_ge(*turn("pe", s))
        ACT.activation(T.cc[:, cols(s)], px(s), AF.Identity, bias=c(BIAS) if s >= K else 0.0, scale=KK).then_inc(turn("cp", s)[0], 1)

    for s in range(1, K):
        addend(s)
    ACT.wait_ge(S.of1a, 1)
    lower(K)
    for s in range(K, NSTEP):
        if s + 1 < NSTEP:
            lower(s + 1)
        addend(s)
    for t in range(ND):
        w = 12 * DIRECT[t][2]
        ACT.wait_ge(S["mm%d" % t], 1)
        ACT.activation(T["fin%d" % t][:], T[DIRECT[t][3]][:, 0:w], AF.Identity, bias=-128.0).then_inc(S["fc%d" % t], 1)

    jobs = sorted([(sum(_frames(k, r)) + K * r, 0, k, r) for k in range(NR) for r in _dests(k)]
                  + [(WLAND[k], 1, k, 0) for k in range(2, NWR)])
    last = 0
    for done, kind, k, r in jobs:
        if kind:
            land(k)
            continue
        if done > last:
            SP.wait_ge(S.vx, vx[done + 1])
            last = done
        f0, n = _frames(k, r)
        SP.dma_start(_obuf(T, k, r)[N + me if r == me else r], T.xx[16 * r:16 * r + 16, cols(f0 + K * r, n)]).then_inc(S["so%d" % k], 16)

    def spread(st):
        PE.wait_ge(S.vx, vx[st + 1])
        for t, (r, s0, n, bank) in enumerate(DIRECT):
            w = 12 * n
            for j in range(8):
                if s0 + (w * (j + 1) - 1) // L == st:
                    if j == 0:
                        for t0 in range(t):
                            if DIRECT[t0][3] == bank:
                                PE.wait_ge(S["fc%d" % t0], 1)
                    s1 = 136 * (r - TOP + 1) + 8 - j
                    ins = PE.matmul(T[bank][:, 0:w], T.sel[:, s1:s1 + 128], T.xw[:, L * s0 + w * j:L * s0 + w * (j + 1)], j == 0, j == 7)
                    if j == 7:
                        ins.then_inc(S["mm%d" % t], 1)

    for s in range(NSTEP + K):
        if s < NSTEP:
            if s in WB:
                PE.wait_ge(S["wl%d" % WB.index(s)], nwl[WB.index(s)])
            p = 16 * min(N, s // K + 1)
            ins = PE.matmul(px(s), T.ident[0:p, :], T.wd[0:p, cols(s)], True, s < K)
            if s >= K:
                PE.wait_ge(*turn("gl", s, K))
                ins = PE.matmul(px(s), T.shift[:], T.lg[:, cols(s)], False, True)
            ins.then_inc(turn("pe", s)[0], 1)
        if s - K >= DIRECT[0][1]:
            spread(s - K)

    def round_out(k):
        g.wait_ge(S["so%d" % k], 16 * len(_dests(k)))
        for n in sorted(set(OUT[k]) - {0}):
            ds = [r for r in range(N) if OUT[k][r] == n]
            buf = _obuf(T, k, ds[0])
            send(ds, _dests(k), lambda d: buf[d], buf[N + me], S["oa%d" % k], buf[0], S["rk%d" % k])

    nst = [0, 0]

    def store(k):
        f0, n = _frames(k, me)
        if n:
            g.wait_ge(S["oa%d" % k], arrivals(range(N), _dests(k)))
            g.dma_start(T.y[:, cols(f0, n)], _obuf(T, k, me)[N:2 * N]).then_inc(S.st, 16)
            nst[0] += 16

    def direct(ts_):
        tr = []
        for t in ts_:
            r = DIRECT[t][0]
            if r == me:
                continue
            es = _deal(T, topo, near, far, me, _together(t))[r]
            g.wait_ge(S["fc%d" % t], 1)
            if r in near[me]:
                tr.append(_xfer(topo, core, T.cores[r], es, S["fa%d" % t], T["fin%d" % t][:], T["fl%d" % t][me]))
            else:
                tr.append(_xfer(topo, core, far[me][r], es, S["rd%d" % t], T["fin%d" % t][:], T["fl%d" % t][0]))
            ls[0] += len(es)
        if tr:
            g.remote_dma_fused(tr, local_sem=S.ls)

    round_out(0)
    round_out(1)
    store(0)
    round_out(2)
    store(1)
    round_out(3)
    round_out(4)
    direct([0, 1])
    direct([2])
    direct([3])
    for k in range(2, NR):
        store(k)
    g.wait_ge(S.ls, ls[0])
    g.wait_ge(S.st, nst[0])

    for t, (r, s0, n, bank) in enumerate(DIRECT):
        if r == me:
            tc = cols(s0 - K * r, n)
            SP.wait_ge(S["fc%d" % t], 1)
            SP.dma_start(T.y[16 * me:16 * me + 16, tc], T["fin%d" % t][:]).then_inc(S.stf, 16)
            SP.wait_ge(S["fa%d" % t], arrivals(range(N), _together(t)))
            runs = _runs([x for x in range(N) if x != me])
            for a, b in runs:
                SP.dma_start(T.y[16 * a:16 * b, tc], T["fl%d" % t][a:b]).then_inc(S.stf, 16)
            nst[1] += 16 * (1 + len(runs))
    if nst[1]:
        SP.wait_ge(S.stf, nst[1])
